import numpy as np
import ml_dtypes


def mxq(x, axis, fmt="e4m3"):
    dtype, down = {"e4m3": (ml_dtypes.float8_e4m3fn, 7), "e5m2": (ml_dtypes.float8_e5m2, 14)}[fmt]
    v = np.moveaxis(np.asarray(x, np.float32).astype(ml_dtypes.bfloat16).astype(np.float64), axis, -1)
    blocks = v.reshape(v.shape[:-1] + (-1, 32))
    amax = np.abs(blocks).max(-1, keepdims=True)
    byte = np.maximum(np.where(amax > 0, np.frexp(amax)[1] - 1 + 127, 0) - down, 1)
    scale = np.exp2(byte - 127.0)
    codes = (blocks / scale).astype(np.float32).astype(dtype).astype(np.float64)
    return np.moveaxis((codes * scale).reshape(v.shape), -1, axis)


WIDE = False


def mx_kscale(k):
    if not WIDE:
        return np.ones(k)
    levels = np.array([10, -10, 5, -5, 0])
    if k % 512:
        return np.exp2(np.random.permutation(np.resize(levels, k // 32))).repeat(32)
    a = np.empty((k // 512, 16))
    for p in range(k // 512):
        a[p, :8] = np.random.permutation(np.resize(levels, 8))
        for g in range(8):
            far = levels[np.abs(levels - a[p, g]) >= 10]
            a[p, g + 8] = far[np.random.randint(len(far))]
    return np.exp2(a.ravel()).repeat(32)


def f64(x):
    return np.asarray(x).astype(np.float64)


def striped(idx):
    return np.tile(idx.reshape(-1, 16).T, (8, 1)).astype(np.uint16)


def unstriped(offs):
    return offs[:16].T.reshape(-1).astype(np.int64)


def pack_weight(w):
    k, n = w.shape
    w = f64(np.asarray(w, np.float32).astype(ml_dtypes.bfloat16)).reshape(k // 32, 32, n)
    amax = np.abs(w).max(1)
    byte = np.clip(np.where(amax > 0, np.frexp(amax)[1] - 1 + 127 - 7, 1), 1, 254)
    scaled = (w * np.exp2(127.0 - byte)[:, None, :]).reshape(k, n).astype(np.float32)
    words = np.ascontiguousarray(scaled.reshape(k // 512, 128, 4, n).transpose(0, 1, 3, 2)).astype(ml_dtypes.float8_e4m3fn).view(np.uint8)
    return words, np.ascontiguousarray(byte.astype(np.uint8).reshape(k // 512, 16, n))


def unpack_weight(words, scales):
    g, p, n, _ = words.shape
    vals = np.ascontiguousarray(words).view(ml_dtypes.float8_e4m3fn).astype(np.float64) * np.repeat(np.exp2(scales.astype(np.float64) - 127.0), 8, axis=1)[..., None]
    return vals.transpose(0, 1, 3, 2).reshape(g * 512, n)


def relu(v):
    return np.maximum(v, 0.0)


K, T, S, V = 512, 1024, 512, 512


def setup_inputs():
    n = np.random.standard_normal
    s = mx_kscale(K)[:, None]
    packed_xT = pack_weight(n((K, T)) * s)
    packed_eT = pack_weight(n((K, T)) * s)
    return {
        "x_words": packed_xT[0],
        "x_scales": packed_xT[1],
        "e_words": packed_eT[0],
        "e_scales": packed_eT[1],
        "hr": (n((K, V)) / np.sqrt(K) / s).astype(np.float32),
        "hi": (n((K, V)) / np.sqrt(K) / s).astype(np.float32),
        "offs": striped(np.random.permutation(T)[:S]),
    }


def reference(x_words, x_scales, e_words, e_scales, hr, hi, offs):
    hrq = mxq(f64(hr), 0, "e4m3")
    xq = unpack_weight(x_words, x_scales)[:, unstriped(offs)]
    hiq = mxq(f64(hi), 0, "e4m3")
    e_offs = unpack_weight(e_words, e_scales)[:, unstriped(offs)]
    z = hiq.T @ e_offs
    re = (hrq.T @ xq) - z
    im = hrq.T @ e_offs + hiq.T @ xq
    pw = (re) ** 2 + (im) ** 2
    near = np.pad(pw, ((0, 0), (2, 0)))[:, :S] + np.pad(pw, ((0, 0), (3, 0)))[:, :S]
    far = np.pad(pw, ((0, 0), (4, 0)))[:, :S] + np.pad(pw, ((0, 0), (5, 0)))[:, :S]
    noise = 0.5 * np.maximum(near, far) + 0.2
    return relu(pw / noise - 1.0)

@@ -1,0 +1,185 @@
+from contextlib import ExitStack
+
+import concourse.mybir as mybir
+
+K, T, S, V = 512, 1024, 512, 512
+FLOPS = 4 * 2 * K * V * S
+
+F32 = mybir.dt.float32
+BF16 = mybir.dt.bfloat16
+I32 = mybir.dt.int32
+U32 = mybir.dt.uint32
+U16 = mybir.dt.uint16
+U8 = mybir.dt.uint8
+FP8X4 = mybir.dt.float8_e4m3fn_x4
+ALU = mybir.AluOpType
+ACT = mybir.ActivationFunctionType
+
+P = 128
+PACK = 4
+BLOCKS = V // P
+PAD = 8
+PIECES = [(0, 1), (1, 1), (2, 2)]
+RELU_ON_SCALAR = (0, 1)
+LAST_CUTS = (0, 256, 512)
+
+
+def tile_picked_ycfar_go_p_kernel(
+    tc, x_words, x_scales, e_words, e_scales, hr, hi, offs, out
+):
+    nc = tc.nc
+    with ExitStack() as ctx:
+        keep = ctx.enter_context(tc.tile_pool(name="keep", bufs=1))
+        psum = ctx.enter_context(tc.psum_pool(name="psum", bufs=1))
+
+        offsets = keep.tile([P, S // 16], U16, name="offsets")
+        xw = keep.tile([P, T], I32, name="xw", align_bytes=64)
+        ew = keep.tile([P, T], I32, name="ew", align_bytes=64)
+        xs = keep.tile([P, T], U8, name="xs", align_bytes=64)
+        es = keep.tile([P, T], U8, name="es", align_bytes=64)
+        xwg = keep.tile([P, S], U32, name="xwg", align_bytes=64)
+        ewg = keep.tile([P, S], U32, name="ewg", align_bytes=64)
+        xsg = keep.tile([P, S], U8, name="xsg", align_bytes=64)
+        esg = keep.tile([P, S], U8, name="esg", align_bytes=64)
+        ones = keep.tile([P, BLOCKS, 2], F32, name="ones")
+        root = keep.tile([P, BLOCKS, S], F32, name="root", align_bytes=64)
+        power = [keep.tile([P, PAD + S], F32, name="power%d" % b, align_bytes=64) for b in range(BLOCKS)]
+
+        nc.vector.memset(xs[:].bitcast(I32), 0)
+        nc.vector.memset(ones[:], 1.0)
+        nc.vector.memset(es[:].bitcast(I32), 0)
+        for b in range(BLOCKS):
+            nc.vector.memset(power[b][:, 0:PAD], 0.0)
+
+        def load_words(tile, words):
+            nc.sync.dma_start(tile[:], words[0].rearrange("p n t -> p (n t)").bitcast(I32))
+
+        def load_scales(queue, tile, scales, q):
+            queue.dma_start(tile[32 * q : 32 * q + 4, :].bitcast(I32), scales[0, 4 * q : 4 * q + 4, :].bitcast(I32))
+
+        raw = {}
+
+        def load_filter(name, h, first, count):
+            tile = keep.tile([P, PACK, count * P], F32, name="raw_%s%d" % (name, first), align_bytes=64)
+            nc.sync.dma_start(tile[:], h[:, first * P : (first + count) * P].rearrange("(p j) w -> p j w", j=PACK))
+            raw[(name, first)] = tile
+
+        nc.sync.dma_start(offsets[:], offs)
+        load_scales(nc.scalar, xs, x_scales, 0)
+        load_scales(nc.scalar, xs, x_scales, 1)
+        load_scales(nc.sync, xs, x_scales, 2)
+        load_scales(nc.sync, xs, x_scales, 3)
+        nc.scalar.activation(root[:, :, 0:2], ones[:], ACT.Abs_reciprocal_sqrt, scale=0.2)
+        load_words(xw, x_words)
+        load_filter("r", hr, *PIECES[0])
+        load_filter("i", hi, *PIECES[0])
+        load_words(ew, e_words)
+        for q in range(4):
+            load_scales(nc.scalar, es, e_scales, q)
+        for piece in PIECES[1:]:
+            load_filter("r", hr, *piece)
+            load_filter("i", hi, *piece)
+
+        codes = {}
+
+        def quantise_piece(first, count):
+            w = count * P
+            both = keep.tile([P, 2, w * PACK], BF16, name="both%d" % first, align_bytes=64)
+            minus = keep.tile([P, w * PACK], BF16, name="minus%d" % first, align_bytes=64)
+            words = keep.tile([P, 2 * w], U32, name="words%d" % first, align_bytes=64)
+            planes = keep.tile([P, 2 * w], U8, name="planes%d" % first, align_bytes=64)
+            mwords = keep.tile([P, w], U32, name="mwords%d" % first, align_bytes=64)
+            mplanes = keep.tile([P, w], U8, name="mplanes%d" % first, align_bytes=64)
+            for n, name in enumerate(("r", "i")):
+                nc.scalar.copy(
+                    both[:, n, :].rearrange("p (c i t) -> p c t i", i=4, t=PACK),
+                    raw[(name, first)][:].rearrange("p t (c i) -> p c t i", i=4),
+                )
+            nc.vector.tensor_scalar(minus[:], both[:, 1, :], -1.0, None, ALU.mult)
+            nc.vector.quantize_mx(words[:].bitcast(FP8X4), planes[:], both[:].rearrange("p n w -> p (n w)"))
+            nc.vector.quantize_mx(mwords[:].bitcast(FP8X4), mplanes[:], minus[:])
+            for b in range(count):
+                lo, hi_ = b * P, (b + 1) * P
+                codes[("r", first + b)] = (words[:, lo:hi_].bitcast(FP8X4), planes[:, lo:hi_])
+                codes[("i", first + b)] = (words[:, w + lo : w + hi_].bitcast(FP8X4), planes[:, w + lo : w + hi_])
+                codes[("m", first + b)] = (mwords[:, lo:hi_].bitcast(FP8X4), mplanes[:, lo:hi_])
+
+        def product(bank, name, b, wg, sg, start):
+            lhs, lhs_scale = codes[(name, b)]
+            nc.tensor.matmul_mx(bank[:], lhsT=lhs, lhsT_scale=lhs_scale, rhs=wg[:].bitcast(FP8X4), rhs_scale=sg[:], start=start, stop=not start)
+
+        nc.vector.tensor_copy(xsg[:], xs[:].indirect(offsets[:]))
+        nc.vector.tensor_copy(xwg[:], xw[:].bitcast(U32).indirect(offsets[:]))
+        quantise_piece(*PIECES[0])
+        nc.vector.tensor_copy(ewg[:], ew[:].bitcast(U32).indirect(offsets[:]))
+        nc.vector.tensor_copy(esg[:], es[:].indirect(offsets[:]))
+        quantise_piece(*PIECES[1])
+
+        def work(name, b):
+            return keep.tile([P, S], F32, name="%s%d" % (name, b), align_bytes=64)
+
+        re2 = [work("re2", b) for b in range(BLOCKS)]
+        im2 = [work("im2", b) for b in range(BLOCKS)]
+        pairs = [work("pairs", b) for b in range(BLOCKS)]
+        big = [work("big", b) for b in range(BLOCKS)]
+        inv = [work("inv", b) for b in range(BLOCKS)]
+        ratio = [work("ratio", b) for b in range(BLOCKS)]
+        res = [work("res", b) for b in range(BLOCKS)]
+        banks = {}
+
+        def multiply(b):
+            re = psum.tile([P, S], F32, name="re%d" % b)
+            im = psum.tile([P, S], F32, name="im%d" % b)
+            product(re, "r", b, xwg, xsg, True)
+            product(im, "i", b, xwg, xsg, True)
+            product(re, "m", b, ewg, esg, False)
+            product(im, "r", b, ewg, esg, False)
+            banks[b] = (re, im)
+
+        def squares(b, lo, hi_):
+            nc.scalar.activation(re2[b][:, lo:hi_], banks[b][0][:, lo:hi_], ACT.Square)
+            nc.scalar.activation(im2[b][:, lo:hi_], banks[b][1][:, lo:hi_], ACT.Square)
+
+        def make_power(b, lo, hi_):
+            nc.vector.tensor_tensor(power[b][:, PAD + lo : PAD + hi_], re2[b][:, lo:hi_], im2[b][:, lo:hi_], ALU.add)
+
+        def make_pairs(b, lo, hi_):
+            nc.vector.scalar_tensor_tensor(pairs[b][:, lo:hi_], power[b][:, PAD - 2 + lo : PAD - 2 + hi_], 0.4, power[b][:, PAD - 3 + lo : PAD - 3 + hi_], ALU.add, ALU.add)
+
+        def make_noise(b, lo, hi_):
+            first = max(lo, 2)
+            nc.vector.tensor_tensor(big[b][:, first:hi_], pairs[b][:, first:hi_], pairs[b][:, first - 2 : hi_ - 2], ALU.max)
+            nc.scalar.activation(root[:, b, first:hi_], big[b][:, first:hi_], ACT.Abs_reciprocal_sqrt, scale=0.5)
+            nc.scalar.activation(inv[b][:, lo:hi_], root[:, b, lo:hi_], ACT.Square)
+
+        def make_ratio(b, lo, hi_):
+            nc.vector.tensor_tensor(ratio[b][:, lo:hi_], power[b][:, PAD + lo : PAD + hi_], inv[b][:, lo:hi_], ALU.mult)
+
+        def finish(b, lo, hi_):
+            if b in RELU_ON_SCALAR:
+                nc.scalar.activation(res[b][:, lo:hi_], ratio[b][:, lo:hi_], ACT.Relu, bias=-1.0)
+            else:
+                nc.vector.tensor_scalar(res[b][:, lo:hi_], ratio[b][:, lo:hi_], -1.0, 0.0, ALU.add, ALU.max)
+            nc.sync.dma_start(out[b * P : (b + 1) * P, lo:hi_], res[b][:, lo:hi_])
+
+        units = [(b, 0, S) for b in range(BLOCKS - 1)]
+        units = units + [(BLOCKS - 1, lo, hi_) for lo, hi_ in zip(LAST_CUTS[:-1], LAST_CUTS[1:])]
+        for u in range(len(units) + 1):
+            now = units[u] if u < len(units) else None
+            before = units[u - 1] if u > 0 else None
+            if now:
+                if now[1] == 0:
+                    multiply(now[0])
+                squares(*now)
+                if u == 0:
+                    for piece in PIECES[2:]:
+                        quantise_piece(*piece)
+                make_power(*now)
+            if before:
+                make_ratio(*before)
+            if now:
+                make_pairs(*now)
+            if before:
+                finish(*before)
+            if now:
+                make_noise(*now)

@@ -20,7 +20,7 @@ PACK = 4
 BLOCKS = V // P
 PAD = 8
 PIECES = [(0, 1), (1, 1), (2, 2)]
-RELU_ON_SCALAR = (0, 1)
+RELU_ON_SCALAR = (1,)
 LAST_CUTS = (0, 256, 512)
 
 
@@ -60,23 +60,19 @@ def tile_picked_ycfar_go_p_kernel(
         raw = {}
 
         def load_filter(name, h, first, count):
-            tile = keep.tile([P, PACK, count * P], F32, name="raw_%s%d" % (name, first), align_bytes=64)
+            tile = keep.tile([P, PACK, count * P], F32, name="raw_%s%d" % (name, first), tag="raw_%s%d" % (name, first), align_bytes=64)
             nc.sync.dma_start(tile[:], h[:, first * P : (first + count) * P].rearrange("(p j) w -> p j w", j=PACK))
             raw[(name, first)] = tile
 
         nc.sync.dma_start(offsets[:], offs)
-        load_scales(nc.scalar, xs, x_scales, 0)
-        load_scales(nc.scalar, xs, x_scales, 1)
-        load_scales(nc.sync, xs, x_scales, 2)
-        load_scales(nc.sync, xs, x_scales, 3)
+        for q in range(4):
+            load_scales(nc.sync if q < 2 else nc.scalar, xs, x_scales, q)
         nc.scalar.activation(root[:, :, 0:2], ones[:], ACT.Abs_reciprocal_sqrt, scale=0.2)
-        load_words(xw, x_words)
-        load_filter("r", hr, *PIECES[0])
-        load_filter("i", hi, *PIECES[0])
-        load_words(ew, e_words)
         for q in range(4):
             load_scales(nc.scalar, es, e_scales, q)
-        for piece in PIECES[1:]:
+        load_words(xw, x_words)
+        load_words(ew, e_words)
+        for piece in PIECES:
             load_filter("r", hr, *piece)
             load_filter("i", hi, *piece)
 
@@ -91,7 +87,8 @@ def tile_picked_ycfar_go_p_kernel(
             mwords = keep.tile([P, w], U32, name="mwords%d" % first, align_bytes=64)
             mplanes = keep.tile([P, w], U8, name="mplanes%d" % first, align_bytes=64)
             for n, name in enumerate(("r", "i")):
-                nc.scalar.copy(
+                copy = nc.vector.tensor_copy if (first, name) == (2, "i") else nc.scalar.copy
+                copy(
                     both[:, n, :].rearrange("p (c i t) -> p c t i", i=4, t=PACK),
                     raw[(name, first)][:].rearrange("p t (c i) -> p c t i", i=4),
                 )
@@ -110,16 +107,15 @@ def tile_picked_ycfar_go_p_kernel(
 
         nc.vector.tensor_copy(xsg[:], xs[:].indirect(offsets[:]))
         nc.vector.tensor_copy(xwg[:], xw[:].bitcast(U32).indirect(offsets[:]))
-        quantise_piece(*PIECES[0])
         nc.vector.tensor_copy(ewg[:], ew[:].bitcast(U32).indirect(offsets[:]))
         nc.vector.tensor_copy(esg[:], es[:].indirect(offsets[:]))
-        quantise_piece(*PIECES[1])
+        for piece in PIECES:
+            quantise_piece(*piece)
 
         def work(name, b):
             return keep.tile([P, S], F32, name="%s%d" % (name, b), align_bytes=64)
 
-        re2 = [work("re2", b) for b in range(BLOCKS)]
-        im2 = [work("im2", b) for b in range(BLOCKS)]
+        re2, im2 = {}, {}
         pairs = [work("pairs", b) for b in range(BLOCKS)]
         big = [work("big", b) for b in range(BLOCKS)]
         inv = [work("inv", b) for b in range(BLOCKS)]
@@ -131,10 +127,12 @@ def tile_picked_ycfar_go_p_kernel(
             re = psum.tile([P, S], F32, name="re%d" % b)
             im = psum.tile([P, S], F32, name="im%d" % b)
             product(re, "r", b, xwg, xsg, True)
-            product(im, "i", b, xwg, xsg, True)
             product(re, "m", b, ewg, esg, False)
+            product(im, "i", b, xwg, xsg, True)
             product(im, "r", b, ewg, esg, False)
             banks[b] = (re, im)
+            sq = keep.tile([P, 2 * S], F32, name="sq%d" % b, tag="raw_r2", align_bytes=64)
+            re2[b], im2[b] = sq[:, 0:S], sq[:, S : 2 * S]
 
         def squares(b, lo, hi_):
             nc.scalar.activation(re2[b][:, lo:hi_], banks[b][0][:, lo:hi_], ACT.Square)
@@ -171,9 +169,6 @@ def tile_picked_ycfar_go_p_kernel(
                 if now[1] == 0:
                     multiply(now[0])
                 squares(*now)
-                if u == 0:
-                    for piece in PIECES[2:]:
-                        quantise_piece(*piece)
                 make_power(*now)
             if before:
                 make_ratio(*before)

@@ -19,8 +19,8 @@ P = 128
 PACK = 4
 BLOCKS = V // P
 PAD = 8
-PIECES = [(0, 1), (1, 1), (2, 2)]
-RELU_ON_SCALAR = (1,)
+PIECES = [(0, 1), (1, 1), (2, 1), (3, 1)]
+RELU_ON_SCALAR = (0, 1)
 LAST_CUTS = (0, 256, 512)
 
 
@@ -65,16 +65,17 @@ def tile_picked_ycfar_go_p_kernel(
             raw[(name, first)] = tile
 
         nc.sync.dma_start(offsets[:], offs)
-        for q in range(4):
-            load_scales(nc.sync if q < 2 else nc.scalar, xs, x_scales, q)
         nc.scalar.activation(root[:, :, 0:2], ones[:], ACT.Abs_reciprocal_sqrt, scale=0.2)
-        for q in range(4):
-            load_scales(nc.scalar, es, e_scales, q)
         load_words(xw, x_words)
+        for q in range(4):
+            load_scales(nc.sync, xs, x_scales, q)
         load_words(ew, e_words)
         for piece in PIECES:
             load_filter("r", hr, *piece)
             load_filter("i", hi, *piece)
+            if piece[0] == 0:
+                for q in range(4):
+                    load_scales(nc.sync, es, e_scales, q)
 
         codes = {}
 
@@ -87,12 +88,20 @@ def tile_picked_ycfar_go_p_kernel(
             mwords = keep.tile([P, w], U32, name="mwords%d" % first, align_bytes=64)
             mplanes = keep.tile([P, w], U8, name="mplanes%d" % first, align_bytes=64)
             for n, name in enumerate(("r", "i")):
-                copy = nc.vector.tensor_copy if (first, name) == (2, "i") else nc.scalar.copy
+                copy = nc.vector.tensor_copy if (first, name) == (3, "i") else nc.scalar.copy
                 copy(
                     both[:, n, :].rearrange("p (c i t) -> p c t i", i=4, t=PACK),
                     raw[(name, first)][:].rearrange("p t (c i) -> p c t i", i=4),
                 )
-            nc.vector.tensor_scalar(minus[:], both[:, 1, :], -1.0, None, ALU.mult)
+            if first == 0:
+                nc.scalar.activation(
+                    minus[:].rearrange("p (c i t) -> p c t i", i=4, t=PACK),
+                    raw[("i", first)][:].rearrange("p t (c i) -> p c t i", i=4),
+                    ACT.Copy,
+                    scale=-1.0,
+                )
+            else:
+                nc.vector.tensor_scalar(minus[:], both[:, 1, :], -1.0, None, ALU.mult)
             nc.vector.quantize_mx(words[:].bitcast(FP8X4), planes[:], both[:].rearrange("p n w -> p (n w)"))
             nc.vector.quantize_mx(mwords[:].bitcast(FP8X4), mplanes[:], minus[:])
             for b in range(count):
@@ -105,11 +114,12 @@ def tile_picked_ycfar_go_p_kernel(
             lhs, lhs_scale = codes[(name, b)]
             nc.tensor.matmul_mx(bank[:], lhsT=lhs, lhsT_scale=lhs_scale, rhs=wg[:].bitcast(FP8X4), rhs_scale=sg[:], start=start, stop=not start)
 
-        nc.vector.tensor_copy(xsg[:], xs[:].indirect(offsets[:]))
         nc.vector.tensor_copy(xwg[:], xw[:].bitcast(U32).indirect(offsets[:]))
+        nc.vector.tensor_copy(xsg[:], xs[:].indirect(offsets[:]))
+        quantise_piece(*PIECES[0])
         nc.vector.tensor_copy(ewg[:], ew[:].bitcast(U32).indirect(offsets[:]))
         nc.vector.tensor_copy(esg[:], es[:].indirect(offsets[:]))
-        for piece in PIECES:
+        for piece in PIECES[1:]:
             quantise_piece(*piece)
 
         def work(name, b):
@@ -131,7 +141,7 @@ def tile_picked_ycfar_go_p_kernel(
             product(im, "i", b, xwg, xsg, True)
             product(im, "r", b, ewg, esg, False)
             banks[b] = (re, im)
-            sq = keep.tile([P, 2 * S], F32, name="sq%d" % b, tag="raw_r2", align_bytes=64)
+            sq = keep.tile([P, 2 * S], F32, name="sq%d" % b, tag="raw_i2" if b == 0 else "sq%d" % b, align_bytes=64)
             re2[b], im2[b] = sq[:, 0:S], sq[:, S : 2 * S]
 
         def squares(b, lo, hi_):

@@ -17,11 +17,10 @@ ACT = mybir.ActivationFunctionType
 
 P = 128
 PACK = 4
-BLOCKS = V // P
+BANDS = V // P
+HALF = S // 2
 PAD = 8
-PIECES = [(0, 1), (1, 1), (2, 1), (3, 1)]
-RELU_ON_SCALAR = (0, 1)
-LAST_CUTS = (0, 256, 512)
+SHARES = {"iwords0":"es"}
 
 
 def tile_picked_ycfar_go_p_kernel(
@@ -32,159 +31,244 @@ def tile_picked_ycfar_go_p_kernel(
         keep = ctx.enter_context(tc.tile_pool(name="keep", bufs=1))
         psum = ctx.enter_context(tc.psum_pool(name="psum", bufs=1))
 
+        def sbuf(name, shape, dtype):
+            return keep.tile(shape, dtype, name=name, tag=SHARES.get(name, name), align_bytes=64)
+
         offsets = keep.tile([P, S // 16], U16, name="offsets")
-        xw = keep.tile([P, T], I32, name="xw", align_bytes=64)
-        ew = keep.tile([P, T], I32, name="ew", align_bytes=64)
-        xs = keep.tile([P, T], U8, name="xs", align_bytes=64)
-        es = keep.tile([P, T], U8, name="es", align_bytes=64)
-        xwg = keep.tile([P, S], U32, name="xwg", align_bytes=64)
-        ewg = keep.tile([P, S], U32, name="ewg", align_bytes=64)
-        xsg = keep.tile([P, S], U8, name="xsg", align_bytes=64)
-        esg = keep.tile([P, S], U8, name="esg", align_bytes=64)
-        ones = keep.tile([P, BLOCKS, 2], F32, name="ones")
-        root = keep.tile([P, BLOCKS, S], F32, name="root", align_bytes=64)
-        power = [keep.tile([P, PAD + S], F32, name="power%d" % b, align_bytes=64) for b in range(BLOCKS)]
+        xw, ew = sbuf("xw", [P, T], I32), sbuf("ew", [P, T], I32)
+        xs, es = sbuf("xs", [P, T], U8), sbuf("es", [P, T], U8)
+        xwg, ewg = sbuf("xwg", [P, S], U32), sbuf("ewg", [P, S], U32)
+        xsg, esg = sbuf("xsg", [P, S], U8), sbuf("esg", [P, S], U8)
+        ones = sbuf("ones", [P, BANDS, 2], F32)
+        root = sbuf("root", [P, BANDS, S], F32)
+        power = [sbuf("power%d" % b, [P, PAD + S], F32) for b in range(BANDS)]
 
         nc.vector.memset(xs[:].bitcast(I32), 0)
         nc.vector.memset(ones[:], 1.0)
         nc.vector.memset(es[:].bitcast(I32), 0)
-        for b in range(BLOCKS):
+        for b in range(BANDS):
             nc.vector.memset(power[b][:, 0:PAD], 0.0)
 
         def load_words(tile, words):
             nc.sync.dma_start(tile[:], words[0].rearrange("p n t -> p (n t)").bitcast(I32))
 
-        def load_scales(queue, tile, scales, q):
-            queue.dma_start(tile[32 * q : 32 * q + 4, :].bitcast(I32), scales[0, 4 * q : 4 * q + 4, :].bitcast(I32))
+        def load_scales(queue, tile, scales):
+            for q in range(4):
+                queue.dma_start(tile[32 * q : 32 * q + 4, :].bitcast(I32), scales[0, 4 * q : 4 * q + 4, :].bitcast(I32))
 
         raw = {}
 
-        def load_filter(name, h, first, count):
-            tile = keep.tile([P, PACK, count * P], F32, name="raw_%s%d" % (name, first), tag="raw_%s%d" % (name, first), align_bytes=64)
-            nc.sync.dma_start(tile[:], h[:, first * P : (first + count) * P].rearrange("(p j) w -> p j w", j=PACK))
-            raw[(name, first)] = tile
+        def load_filter(name, h, b):
+            raw[name, b] = sbuf("raw_%s%d" % (name, b), [P, PACK, P], F32)
+            nc.sync.dma_start(raw[name, b][:], h[:, b * P : (b + 1) * P].rearrange("(p j) w -> p j w", j=PACK))
 
         nc.sync.dma_start(offsets[:], offs)
         nc.scalar.activation(root[:, :, 0:2], ones[:], ACT.Abs_reciprocal_sqrt, scale=0.2)
         load_words(xw, x_words)
-        for q in range(4):
-            load_scales(nc.sync, xs, x_scales, q)
+        load_scales(nc.sync, xs, x_scales)
+        load_filter("r", hr, 0)
+        load_filter("i", hi, 0)
+        load_scales(nc.sync, es, e_scales)
         load_words(ew, e_words)
-        for piece in PIECES:
-            load_filter("r", hr, *piece)
-            load_filter("i", hi, *piece)
-            if piece[0] == 0:
-                for q in range(4):
-                    load_scales(nc.sync, es, e_scales, q)
+        load_filter("r", hr, 1)
+        load_filter("i", hi, 1)
+        load_filter("r", hr, 2)
+        load_filter("i", hi, 2)
+        load_filter("r", hr, 3)
+        load_filter("i", hi, 3)
 
         codes = {}
 
-        def quantise_piece(first, count):
-            w = count * P
-            both = keep.tile([P, 2, w * PACK], BF16, name="both%d" % first, align_bytes=64)
-            minus = keep.tile([P, w * PACK], BF16, name="minus%d" % first, align_bytes=64)
-            words = keep.tile([P, 2 * w], U32, name="words%d" % first, align_bytes=64)
-            planes = keep.tile([P, 2 * w], U8, name="planes%d" % first, align_bytes=64)
-            mwords = keep.tile([P, w], U32, name="mwords%d" % first, align_bytes=64)
-            mplanes = keep.tile([P, w], U8, name="mplanes%d" % first, align_bytes=64)
-            for n, name in enumerate(("r", "i")):
-                copy = nc.vector.tensor_copy if (first, name) == (3, "i") else nc.scalar.copy
-                copy(
-                    both[:, n, :].rearrange("p (c i t) -> p c t i", i=4, t=PACK),
-                    raw[(name, first)][:].rearrange("p t (c i) -> p c t i", i=4),
-                )
-            if first == 0:
-                nc.scalar.activation(
-                    minus[:].rearrange("p (c i t) -> p c t i", i=4, t=PACK),
-                    raw[("i", first)][:].rearrange("p t (c i) -> p c t i", i=4),
-                    ACT.Copy,
-                    scale=-1.0,
-                )
+        real = [sbuf("real%d" % b, [P, P * PACK], BF16) for b in range(BANDS)]
+        imag = [sbuf("imag%d" % b, [P, 2, P * PACK], BF16) for b in range(BANDS)]
+
+        def interleaved(tile):
+            return tile.rearrange("p (c i t) -> p c t i", i=4, t=PACK)
+
+        def rows(name, b):
+            return raw[name, b][:].rearrange("p t (c i) -> p c t i", i=4)
+
+        def round_filter(engine, name, b):
+            target = interleaved(real[b][:] if name == "r" else imag[b][:, 0, :])
+            if engine == "v":
+                nc.vector.tensor_copy(target, rows(name, b))
+            elif engine == "g":
+                nc.gpsimd.tensor_scalar(target, rows(name, b), 1.0, 0.0, ALU.mult, ALU.add)
             else:
-                nc.vector.tensor_scalar(minus[:], both[:, 1, :], -1.0, None, ALU.mult)
-            nc.vector.quantize_mx(words[:].bitcast(FP8X4), planes[:], both[:].rearrange("p n w -> p (n w)"))
-            nc.vector.quantize_mx(mwords[:].bitcast(FP8X4), mplanes[:], minus[:])
-            for b in range(count):
-                lo, hi_ = b * P, (b + 1) * P
-                codes[("r", first + b)] = (words[:, lo:hi_].bitcast(FP8X4), planes[:, lo:hi_])
-                codes[("i", first + b)] = (words[:, w + lo : w + hi_].bitcast(FP8X4), planes[:, w + lo : w + hi_])
-                codes[("m", first + b)] = (mwords[:, lo:hi_].bitcast(FP8X4), mplanes[:, lo:hi_])
+                nc.scalar.copy(target, rows(name, b))
 
-        def product(bank, name, b, wg, sg, start):
-            lhs, lhs_scale = codes[(name, b)]
-            nc.tensor.matmul_mx(bank[:], lhsT=lhs, lhsT_scale=lhs_scale, rhs=wg[:].bitcast(FP8X4), rhs_scale=sg[:], start=start, stop=not start)
+        def negate(engine, b):
+            if engine == "v":
+                nc.vector.tensor_scalar(imag[b][:, 1, :], imag[b][:, 0, :], -1.0, None, ALU.mult)
+            elif engine == "g":
+                nc.gpsimd.tensor_scalar(interleaved(imag[b][:, 1, :]), rows("i", b), -1.0, 0.0, ALU.mult, ALU.add)
+            else:
+                nc.scalar.activation(interleaved(imag[b][:, 1, :]), rows("i", b), ACT.Copy, scale=-1.0)
 
-        nc.vector.tensor_copy(xwg[:], xw[:].bitcast(U32).indirect(offsets[:]))
-        nc.vector.tensor_copy(xsg[:], xs[:].indirect(offsets[:]))
-        quantise_piece(*PIECES[0])
-        nc.vector.tensor_copy(ewg[:], ew[:].bitcast(U32).indirect(offsets[:]))
-        nc.vector.tensor_copy(esg[:], es[:].indirect(offsets[:]))
-        for piece in PIECES[1:]:
-            quantise_piece(*piece)
+        def quantise(b):
+            words = sbuf("rwords%d" % b, [P, P], U32)
+            planes = sbuf("rplanes%d" % b, [P, P], U8)
+            nc.vector.quantize_mx(words[:].bitcast(FP8X4), planes[:], real[b][:])
+            codes["r", b] = (words[:].bitcast(FP8X4), planes[:])
 
-        def work(name, b):
-            return keep.tile([P, S], F32, name="%s%d" % (name, b), align_bytes=64)
+        def quantise_minus(b):
+            words = sbuf("iwords%d" % b, [P, 2 * P], U32)
+            planes = sbuf("iplanes%d" % b, [P, 2 * P], U8)
+            nc.vector.quantize_mx(words[:].bitcast(FP8X4), planes[:], imag[b][:].rearrange("p n w -> p (n w)"))
+            codes["i", b] = (words[:, 0:P].bitcast(FP8X4), planes[:, 0:P])
+            codes["m", b] = (words[:, P : 2 * P].bitcast(FP8X4), planes[:, P : 2 * P])
 
-        re2, im2 = {}, {}
-        pairs = [work("pairs", b) for b in range(BLOCKS)]
-        big = [work("big", b) for b in range(BLOCKS)]
-        inv = [work("inv", b) for b in range(BLOCKS)]
-        ratio = [work("ratio", b) for b in range(BLOCKS)]
-        res = [work("res", b) for b in range(BLOCKS)]
+        def gather(picked, window, lo, up):
+            nc.vector.tensor_copy(picked[:, lo:up], window.indirect(offsets[:, lo // 16 : up // 16]))
+
+
+        squares = [sbuf("squares%d" % b, [P, 2, 2, HALF], F32) for b in range(BANDS)]
+        pairs = [sbuf("pairs%d" % b, [P, S], F32) for b in range(BANDS)]
+        big = [sbuf("big%d" % b, [P, S], F32) for b in range(BANDS)]
+        inv = [sbuf("inv%d" % b, [P, S], F32) for b in range(BANDS)]
+        ratio = [sbuf("ratio%d" % b, [P, S], F32) for b in range(BANDS)]
+        res = [sbuf("res%d" % b, [P, S], F32) for b in range(BANDS)]
+
         banks = {}
 
-        def multiply(b):
-            re = psum.tile([P, S], F32, name="re%d" % b)
-            im = psum.tile([P, S], F32, name="im%d" % b)
-            product(re, "r", b, xwg, xsg, True)
-            product(re, "m", b, ewg, esg, False)
-            product(im, "i", b, xwg, xsg, True)
-            product(im, "r", b, ewg, esg, False)
-            banks[b] = (re, im)
-            sq = keep.tile([P, 2 * S], F32, name="sq%d" % b, tag="raw_i2" if b == 0 else "sq%d" % b, align_bytes=64)
-            re2[b], im2[b] = sq[:, 0:S], sq[:, S : 2 * S]
+        def multiply_part(b, h, table):
+            if table == 0:
+                banks[b, h] = psum.tile([P, 2, HALF], F32, name="bank%d_%d" % (b, h))
+            cols = slice(h * HALF, (h + 1) * HALF)
+            picked_words, picked_scales = ((xwg, xsg), (ewg, esg))[table]
+            for n, (name, part) in enumerate(((("r", 0), ("i", 1)), (("r", 1), ("m", 0)))[table]):
+                lhs, lhs_scale = codes[name, b]
+                nc.tensor.matmul_mx(
+                    banks[b, h][:, part, :], lhsT=lhs, lhsT_scale=lhs_scale,
+                    rhs=picked_words[:, cols].bitcast(FP8X4), rhs_scale=picked_scales[:, cols],
+                    start=(table, n) == (0, 0), stop=(table, n) == (1, 1),
+                )
 
-        def squares(b, lo, hi_):
-            nc.scalar.activation(re2[b][:, lo:hi_], banks[b][0][:, lo:hi_], ACT.Square)
-            nc.scalar.activation(im2[b][:, lo:hi_], banks[b][1][:, lo:hi_], ACT.Square)
+        def multiply(b, h):
+            multiply_part(b, h, 0)
+            multiply_part(b, h, 1)
 
-        def make_power(b, lo, hi_):
-            nc.vector.tensor_tensor(power[b][:, PAD + lo : PAD + hi_], re2[b][:, lo:hi_], im2[b][:, lo:hi_], ALU.add)
+        def square(b, h):
+            bank = banks[b, h]
+            nc.scalar.activation(squares[b][:, h, :, :], bank[:], ACT.Square)
 
-        def make_pairs(b, lo, hi_):
-            nc.vector.scalar_tensor_tensor(pairs[b][:, lo:hi_], power[b][:, PAD - 2 + lo : PAD - 2 + hi_], 0.4, power[b][:, PAD - 3 + lo : PAD - 3 + hi_], ALU.add, ALU.add)
+        def make_power(b, lo, up):
+            halves = slice(lo // HALF, up // HALF)
+            nc.vector.tensor_tensor(
+                power[b][:, PAD + lo : PAD + up].rearrange("p (h c) -> p h c", c=HALF),
+                squares[b][:, halves, 0, :], squares[b][:, halves, 1, :], ALU.add,
+            )
 
-        def make_noise(b, lo, hi_):
+        def make_pairs(b, lo, up):
+            nc.vector.scalar_tensor_tensor(pairs[b][:, lo:up], power[b][:, PAD - 2 + lo : PAD - 2 + up], 0.4, power[b][:, PAD - 3 + lo : PAD - 3 + up], ALU.add, ALU.add)
+
+        def make_noise(b, lo, up):
             first = max(lo, 2)
-            nc.vector.tensor_tensor(big[b][:, first:hi_], pairs[b][:, first:hi_], pairs[b][:, first - 2 : hi_ - 2], ALU.max)
-            nc.scalar.activation(root[:, b, first:hi_], big[b][:, first:hi_], ACT.Abs_reciprocal_sqrt, scale=0.5)
-            nc.scalar.activation(inv[b][:, lo:hi_], root[:, b, lo:hi_], ACT.Square)
+            nc.vector.tensor_tensor(big[b][:, first:up], pairs[b][:, first:up], pairs[b][:, first - 2 : up - 2], ALU.max)
 
-        def make_ratio(b, lo, hi_):
-            nc.vector.tensor_tensor(ratio[b][:, lo:hi_], power[b][:, PAD + lo : PAD + hi_], inv[b][:, lo:hi_], ALU.mult)
+        def make_inverse(b, lo, up):
+            first = max(lo, 2)
+            nc.scalar.activation(root[:, b, first:up], big[b][:, first:up], ACT.Abs_reciprocal_sqrt, scale=0.5)
 
-        def finish(b, lo, hi_):
-            if b in RELU_ON_SCALAR:
-                nc.scalar.activation(res[b][:, lo:hi_], ratio[b][:, lo:hi_], ACT.Relu, bias=-1.0)
+        def make_inverse2(b, lo, up):
+            nc.scalar.activation(inv[b][:, lo:up], root[:, b, lo:up], ACT.Square)
+
+        def make_ratio(b, lo, up):
+            nc.vector.tensor_tensor(ratio[b][:, lo:up], power[b][:, PAD + lo : PAD + up], inv[b][:, lo:up], ALU.mult)
+
+        def finish(engine, b, lo, up):
+            if engine == "v":
+                nc.vector.tensor_scalar(res[b][:, lo:up], ratio[b][:, lo:up], -1.0, 0.0, ALU.add, ALU.max)
             else:
-                nc.vector.tensor_scalar(res[b][:, lo:hi_], ratio[b][:, lo:hi_], -1.0, 0.0, ALU.add, ALU.max)
-            nc.sync.dma_start(out[b * P : (b + 1) * P, lo:hi_], res[b][:, lo:hi_])
+                nc.scalar.activation(res[b][:, lo:up], ratio[b][:, lo:up], ACT.Relu, bias=-1.0)
+            nc.sync.dma_start(out[b * P : (b + 1) * P, lo:up], res[b][:, lo:up])
 
-        units = [(b, 0, S) for b in range(BLOCKS - 1)]
-        units = units + [(BLOCKS - 1, lo, hi_) for lo, hi_ in zip(LAST_CUTS[:-1], LAST_CUTS[1:])]
-        for u in range(len(units) + 1):
-            now = units[u] if u < len(units) else None
-            before = units[u - 1] if u > 0 else None
-            if now:
-                if now[1] == 0:
-                    multiply(now[0])
-                squares(*now)
-                make_power(*now)
-            if before:
-                make_ratio(*before)
-            if now:
-                make_pairs(*now)
-            if before:
-                finish(*before)
-            if now:
-                make_noise(*now)
+        def products(b, lo, up):
+            for h in range(lo // HALF, up // HALF):
+                multiply(b, h)
+
+        gather(xwg, xw[:].bitcast(U32), 0, S)
+        gather(xsg, xs[:], 0, S)
+        round_filter("s", "r", 0)
+        round_filter("s", "i", 0)
+        negate("s", 0)
+        quantise(0)
+        gather(esg, es[:], 0, S)
+        quantise_minus(0)
+        multiply_part(0, 0, 0)
+        gather(ewg, ew[:].bitcast(U32), 0, HALF)
+        multiply_part(0, 0, 1)
+        multiply_part(0, 1, 0)
+        gather(ewg, ew[:].bitcast(U32), HALF, S)
+        multiply_part(0, 1, 1)
+        round_filter("s", "r", 1)
+        round_filter("v", "i", 1)
+        quantise(1)
+        negate("v", 1)
+        quantise_minus(1)
+        multiply(1, 0)
+        multiply(1, 1)
+        square(0, 0)
+        make_power(0, 0, HALF)
+        make_pairs(0, 0, HALF)
+        round_filter("s", "r", 2)
+        round_filter("v", "i", 2)
+        quantise(2)
+        negate("v", 2)
+        quantise_minus(2)
+        multiply(2, 0)
+        multiply(2, 1)
+        square(0, 1)
+        make_power(0, HALF, S)
+        make_noise(0, 0, HALF)
+        make_inverse(0, 0, HALF)
+        make_pairs(0, HALF, S)
+        make_inverse2(0, 0, HALF)
+        round_filter("s", "r", 3)
+        round_filter("v", "i", 3)
+        quantise(3)
+        negate("v", 3)
+        quantise_minus(3)
+        multiply(3, 0)
+        multiply(3, 1)
+        square(1, 0)
+        square(1, 1)
+        make_power(1, 0, S)
+        make_noise(0, HALF, S)
+        make_inverse(0, HALF, S)
+        make_pairs(1, 0, S)
+        make_inverse2(0, HALF, S)
+        square(2, 0)
+        square(2, 1)
+        make_power(2, 0, S)
+        make_noise(1, 0, S)
+        make_inverse(1, 0, S)
+        make_pairs(2, 0, S)
+        make_inverse2(1, 0, S)
+        make_ratio(0, 0, HALF)
+        square(3, 0)
+        make_power(3, 0, HALF)
+        make_noise(2, 0, S)
+        make_inverse(2, 0, S)
+        make_pairs(3, 0, HALF)
+        make_inverse2(2, 0, S)
+        make_ratio(0, HALF, S)
+        finish("s", 0, 0, HALF)
+        square(3, 1)
+        make_power(3, HALF, S)
+        make_noise(3, 0, HALF)
+        make_inverse(3, 0, HALF)
+        make_pairs(3, HALF, S)
+        make_inverse2(3, 0, HALF)
+        make_ratio(1, 0, S)
+        finish("s", 0, HALF, S)
+        make_noise(3, HALF, S)
+        make_inverse(3, HALF, S)
+        make_inverse2(3, HALF, S)
+        make_ratio(2, 0, S)
+        finish("s", 1, 0, S)
+        make_ratio(3, 0, HALF)
+        finish("v", 2, 0, S)
+        make_ratio(3, HALF, S)
+        finish("v", 3, 0, HALF)
+        finish("v", 3, HALF, S)

@@ -1,6 +1,7 @@
 from contextlib import ExitStack
 
 import concourse.mybir as mybir
+from concourse.masks import make_identity
 
 K, T, S, V = 512, 1024, 512, 512
 FLOPS = 4 * 2 * K * V * S
@@ -19,8 +20,9 @@ P = 128
 PACK = 4
 BANDS = V // P
 HALF = S // 2
-PAD = 8
-SHARES = {"iwords0":"es"}
+PAD = 4
+SHARES = {"squares0":"raw_r2"}
+BANKS = {"product0_0":0,"product0_1":1,"product1_0":2,"product1_1":3,"product2_0":4,"product2_1":5,"product3_0":0,"product3_1":1,"low1":6,"high1":7,"power1":2}
 
 
 def tile_picked_ycfar_go_p_kernel(
@@ -34,27 +36,32 @@ def tile_picked_ycfar_go_p_kernel(
         def sbuf(name, shape, dtype):
             return keep.tile(shape, dtype, name=name, tag=SHARES.get(name, name), align_bytes=64)
 
+        def bank(name):
+            return psum.tile([P, S], F32, name=name, tag="bank%d" % BANKS[name])
+
         offsets = keep.tile([P, S // 16], U16, name="offsets")
         xw, ew = sbuf("xw", [P, T], I32), sbuf("ew", [P, T], I32)
         xs, es = sbuf("xs", [P, T], U8), sbuf("es", [P, T], U8)
         xwg, ewg = sbuf("xwg", [P, S], U32), sbuf("ewg", [P, S], U32)
         xsg, esg = sbuf("xsg", [P, S], U8), sbuf("esg", [P, S], U8)
-        ones = sbuf("ones", [P, BANDS, 2], F32)
-        root = sbuf("root", [P, BANDS, S], F32)
+        ones = sbuf("ones", [P, BANDS, PAD], F32)
+        root = sbuf("root", [P, BANDS, PAD + S], F32)
+        ident = sbuf("ident", [P, P], F32)
         power = [sbuf("power%d" % b, [P, PAD + S], F32) for b in range(BANDS)]
 
         nc.vector.memset(xs[:].bitcast(I32), 0)
         nc.vector.memset(ones[:], 1.0)
         nc.vector.memset(es[:].bitcast(I32), 0)
-        for b in range(BANDS):
+        for b in (0, 2, 3):
             nc.vector.memset(power[b][:, 0:PAD], 0.0)
+        make_identity(nc, ident[:])
 
         def load_words(tile, words):
             nc.sync.dma_start(tile[:], words[0].rearrange("p n t -> p (n t)").bitcast(I32))
 
-        def load_scales(queue, tile, scales):
+        def load_scales(tile, scales):
             for q in range(4):
-                queue.dma_start(tile[32 * q : 32 * q + 4, :].bitcast(I32), scales[0, 4 * q : 4 * q + 4, :].bitcast(I32))
+                nc.sync.dma_start(tile[32 * q : 32 * q + 4, :].bitcast(I32), scales[0, 4 * q : 4 * q + 4, :].bitcast(I32))
 
         raw = {}
 
@@ -63,13 +70,13 @@ def tile_picked_ycfar_go_p_kernel(
             nc.sync.dma_start(raw[name, b][:], h[:, b * P : (b + 1) * P].rearrange("(p j) w -> p j w", j=PACK))
 
         nc.sync.dma_start(offsets[:], offs)
-        nc.scalar.activation(root[:, :, 0:2], ones[:], ACT.Abs_reciprocal_sqrt, scale=0.2)
+        nc.scalar.activation(root[:, :, 0:PAD], ones[:], ACT.Abs_reciprocal_sqrt, scale=0.2)
         load_words(xw, x_words)
-        load_scales(nc.sync, xs, x_scales)
+        load_scales(xs, x_scales)
         load_filter("r", hr, 0)
         load_filter("i", hi, 0)
-        load_scales(nc.sync, es, e_scales)
         load_words(ew, e_words)
+        load_scales(es, e_scales)
         load_filter("r", hr, 1)
         load_filter("i", hi, 1)
         load_filter("r", hr, 2)
@@ -77,10 +84,9 @@ def tile_picked_ycfar_go_p_kernel(
         load_filter("r", hr, 3)
         load_filter("i", hi, 3)
 
-        codes = {}
-
-        real = [sbuf("real%d" % b, [P, P * PACK], BF16) for b in range(BANDS)]
-        imag = [sbuf("imag%d" % b, [P, 2, P * PACK], BF16) for b in range(BANDS)]
+        rounded = [sbuf("rounded%d" % b, [P, 3, P * PACK], BF16) for b in range(BANDS)]
+        words = [sbuf("words%d" % b, [P, 3 * P], U32) for b in range(BANDS)]
+        planes = [sbuf("planes%d" % b, [P, 3 * P], U8) for b in range(BANDS)]
 
         def interleaved(tile):
             return tile.rearrange("p (c i t) -> p c t i", i=4, t=PACK)
@@ -89,92 +95,117 @@ def tile_picked_ycfar_go_p_kernel(
             return raw[name, b][:].rearrange("p t (c i) -> p c t i", i=4)
 
         def round_filter(engine, name, b):
-            target = interleaved(real[b][:] if name == "r" else imag[b][:, 0, :])
-            if engine == "v":
-                nc.vector.tensor_copy(target, rows(name, b))
-            elif engine == "g":
-                nc.gpsimd.tensor_scalar(target, rows(name, b), 1.0, 0.0, ALU.mult, ALU.add)
-            else:
-                nc.scalar.copy(target, rows(name, b))
+            copy = nc.vector.tensor_copy if engine == "v" else nc.scalar.copy
+            copy(interleaved(rounded[b][:, "mri".index(name), :]), rows(name, b))
 
         def negate(engine, b):
             if engine == "v":
-                nc.vector.tensor_scalar(imag[b][:, 1, :], imag[b][:, 0, :], -1.0, None, ALU.mult)
-            elif engine == "g":
-                nc.gpsimd.tensor_scalar(interleaved(imag[b][:, 1, :]), rows("i", b), -1.0, 0.0, ALU.mult, ALU.add)
+                nc.vector.tensor_scalar(rounded[b][:, 0, :], rounded[b][:, 2, :], -1.0, None, ALU.mult)
             else:
-                nc.scalar.activation(interleaved(imag[b][:, 1, :]), rows("i", b), ACT.Copy, scale=-1.0)
+                nc.scalar.activation(interleaved(rounded[b][:, 0, :]), rows("i", b), ACT.Copy, scale=-1.0)
 
-        def quantise(b):
-            words = sbuf("rwords%d" % b, [P, P], U32)
-            planes = sbuf("rplanes%d" % b, [P, P], U8)
-            nc.vector.quantize_mx(words[:].bitcast(FP8X4), planes[:], real[b][:])
-            codes["r", b] = (words[:].bitcast(FP8X4), planes[:])
-
-        def quantise_minus(b):
-            words = sbuf("iwords%d" % b, [P, 2 * P], U32)
-            planes = sbuf("iplanes%d" % b, [P, 2 * P], U8)
-            nc.vector.quantize_mx(words[:].bitcast(FP8X4), planes[:], imag[b][:].rearrange("p n w -> p (n w)"))
-            codes["i", b] = (words[:, 0:P].bitcast(FP8X4), planes[:, 0:P])
-            codes["m", b] = (words[:, P : 2 * P].bitcast(FP8X4), planes[:, P : 2 * P])
+        def quantise(b, first, count):
+            cols = slice(first * P, (first + count) * P)
+            nc.vector.quantize_mx(words[b][:, cols].bitcast(FP8X4), planes[b][:, cols], rounded[b][:, first : first + count, :].rearrange("p n w -> p (n w)"))
 
         def gather(picked, window, lo, up):
             nc.vector.tensor_copy(picked[:, lo:up], window.indirect(offsets[:, lo // 16 : up // 16]))
 
-
-        squares = [sbuf("squares%d" % b, [P, 2, 2, HALF], F32) for b in range(BANDS)]
+        squares = [sbuf("squares%d" % b, [P, 2 * S], F32) for b in range(BANDS)]
         pairs = [sbuf("pairs%d" % b, [P, S], F32) for b in range(BANDS)]
-        big = [sbuf("big%d" % b, [P, S], F32) for b in range(BANDS)]
+        least = [sbuf("least%d" % b, [P, S], F32) for b in range(BANDS)]
         inv = [sbuf("inv%d" % b, [P, S], F32) for b in range(BANDS)]
         ratio = [sbuf("ratio%d" % b, [P, S], F32) for b in range(BANDS)]
         res = [sbuf("res%d" % b, [P, S], F32) for b in range(BANDS)]
+        picked = ((xwg, xsg), (ewg, esg))
+        held = {}
 
-        banks = {}
-
-        def multiply_part(b, h, table):
+        def filters_stationary(b, h, table):
             if table == 0:
-                banks[b, h] = psum.tile([P, 2, HALF], F32, name="bank%d_%d" % (b, h))
+                held["product", b, h] = bank("product%d_%d" % (b, h))
             cols = slice(h * HALF, (h + 1) * HALF)
-            picked_words, picked_scales = ((xwg, xsg), (ewg, esg))[table]
-            for n, (name, part) in enumerate(((("r", 0), ("i", 1)), (("r", 1), ("m", 0)))[table]):
-                lhs, lhs_scale = codes[name, b]
+            for part in range(2):
+                mine = slice((1 - table + part) * P, (2 - table + part) * P)
                 nc.tensor.matmul_mx(
-                    banks[b, h][:, part, :], lhsT=lhs, lhsT_scale=lhs_scale,
-                    rhs=picked_words[:, cols].bitcast(FP8X4), rhs_scale=picked_scales[:, cols],
-                    start=(table, n) == (0, 0), stop=(table, n) == (1, 1),
+                    held["product", b, h][:, part * HALF : (part + 1) * HALF],
+                    lhsT=words[b][:, mine].bitcast(FP8X4), lhsT_scale=planes[b][:, mine],
+                    rhs=picked[table][0][:, cols].bitcast(FP8X4), rhs_scale=picked[table][1][:, cols],
+                    start=(table, part) == (0, 0), stop=(table, part) == (1, 1),
                 )
 
-        def multiply(b, h):
-            multiply_part(b, h, 0)
-            multiply_part(b, h, 1)
+        def bins_stationary(b, h, table):
+            if table == 0:
+                held["product", b, h] = bank("product%d_%d" % (b, h))
+            mine = slice((1 - table) * P, (3 - table) * P)
+            for block in range(2):
+                cols = slice((2 * h + block) * P, (2 * h + block + 1) * P)
+                nc.tensor.matmul_mx(
+                    held["product", b, h][:, block * 2 * P : (block + 1) * 2 * P],
+                    lhsT=picked[table][0][:, cols].bitcast(FP8X4), lhsT_scale=picked[table][1][:, cols],
+                    rhs=words[b][:, mine].bitcast(FP8X4), rhs_scale=planes[b][:, mine],
+                    start=(table, block) == (0, 0), stop=(table, block) == (1, 1),
+                )
 
-        def square(b, h):
-            bank = banks[b, h]
-            nc.scalar.activation(squares[b][:, h, :, :], bank[:], ACT.Square)
+        def square_rows(b, h):
+            target = squares[b][:].rearrange("p (part s) -> p part s", part=2)[:, :, h * HALF : (h + 1) * HALF]
+            nc.scalar.activation(target, held["product", b, h][:].rearrange("p (part s) -> p part s", part=2), ACT.Square)
 
-        def make_power(b, lo, up):
-            halves = slice(lo // HALF, up // HALF)
-            nc.vector.tensor_tensor(
-                power[b][:, PAD + lo : PAD + up].rearrange("p (h c) -> p h c", c=HALF),
-                squares[b][:, halves, 0, :], squares[b][:, halves, 1, :], ALU.add,
-            )
+        def square_bins(b, h):
+            nc.scalar.activation(squares[b][:, h * S : (h + 1) * S], held["product", b, h][:], ACT.Square)
+
+        def add_rows(b, lo, up):
+            nc.vector.tensor_tensor(power[b][:, PAD + lo : PAD + up], squares[b][:, lo:up], squares[b][:, S + lo : S + up], ALU.add)
+
+        def add_bins(b):
+            parts = squares[b][:].rearrange("p (block part t) -> p block part t", part=2, t=P)
+            nc.vector.tensor_tensor(power[b][:, 0:S].rearrange("p (block t) -> p block t", t=P), parts[:, :, 0, :], parts[:, :, 1, :], ALU.add)
+
+        def turn(name, b, passes, sources):
+            held[name, b] = bank("%s%d" % (name, b))
+            total = len(passes) * len(sources)
+            for n, (block, column) in enumerate(passes):
+                for k, source in enumerate(sources):
+                    nc.tensor.matmul(
+                        held[name, b][:, column : column + P], source(block), ident[:],
+                        start=n * len(sources) + k == 0, stop=n * len(sources) + k == total - 1, is_transpose=True,
+                    )
+
+        def summed(b):
+            return [lambda block: power[b][:, block * P : (block + 1) * P]]
+
+        def unsummed(b):
+            return [lambda block, part=part: squares[b][:, (2 * block + part) * P : (2 * block + part + 1) * P] for part in range(2)]
+
+        def turn_power(b, sources):
+            turn("power", b, [(block, block * P) for block in range(4)], sources)
+
+        def turn_low(b, sources):
+            turn("low", b, [(block, block * P) for block in range(3)] + [(block, block * P + 1) for block in range(2)], sources)
+
+        def turn_high(b, sources):
+            turn("high", b, [(block, (block - 1) * P) for block in (1, 2, 3)] + [(block, (block - 1) * P - 1) for block in (2, 3)], sources)
+
+        def root_low(b):
+            nc.scalar.activation(root[:, b, PAD : PAD + HALF], held["low", b][:, 0:HALF], ACT.Abs_reciprocal_sqrt, bias=0.2, scale=0.5)
+
+        def root_high(b):
+            nc.scalar.activation(root[:, b, PAD + HALF : PAD + S - 2], held["high", b][:, P - 1 : P - 1 + HALF - 2], ACT.Abs_reciprocal_sqrt, bias=0.2, scale=0.5)
 
         def make_pairs(b, lo, up):
-            nc.vector.scalar_tensor_tensor(pairs[b][:, lo:up], power[b][:, PAD - 2 + lo : PAD - 2 + up], 0.4, power[b][:, PAD - 3 + lo : PAD - 3 + up], ALU.add, ALU.add)
+            nc.vector.tensor_tensor(pairs[b][:, lo:up], power[b][:, PAD + lo : PAD + up], power[b][:, PAD - 1 + lo : PAD - 1 + up], ALU.add)
 
-        def make_noise(b, lo, up):
-            first = max(lo, 2)
-            nc.vector.tensor_tensor(big[b][:, first:up], pairs[b][:, first:up], pairs[b][:, first - 2 : up - 2], ALU.max)
+        def root_rows(b, lo, up):
+            nc.scalar.activation(root[:, b, PAD + lo : PAD + up], pairs[b][:, lo:up], ACT.Abs_reciprocal_sqrt, bias=0.2, scale=0.5)
+
+        def make_least(b, lo, up):
+            nc.vector.tensor_tensor(least[b][:, lo:up], root[:, b, PAD - 2 + lo : PAD - 2 + up], root[:, b, PAD - 4 + lo : PAD - 4 + up], ALU.min)
 
         def make_inverse(b, lo, up):
-            first = max(lo, 2)
-            nc.scalar.activation(root[:, b, first:up], big[b][:, first:up], ACT.Abs_reciprocal_sqrt, scale=0.5)
-
-        def make_inverse2(b, lo, up):
-            nc.scalar.activation(inv[b][:, lo:up], root[:, b, lo:up], ACT.Square)
+            nc.scalar.activation(inv[b][:, lo:up], least[b][:, lo:up], ACT.Square)
 
         def make_ratio(b, lo, up):
-            nc.vector.tensor_tensor(ratio[b][:, lo:up], power[b][:, PAD + lo : PAD + up], inv[b][:, lo:up], ALU.mult)
+            source = held["power", b][:, lo:up] if ("power", b) in held else power[b][:, PAD + lo : PAD + up]
+            nc.vector.tensor_tensor(ratio[b][:, lo:up], source, inv[b][:, lo:up], ALU.mult)
 
         def finish(engine, b, lo, up):
             if engine == "v":
@@ -183,92 +214,89 @@ def tile_picked_ycfar_go_p_kernel(
                 nc.scalar.activation(res[b][:, lo:up], ratio[b][:, lo:up], ACT.Relu, bias=-1.0)
             nc.sync.dma_start(out[b * P : (b + 1) * P, lo:up], res[b][:, lo:up])
 
-        def products(b, lo, up):
-            for h in range(lo // HALF, up // HALF):
-                multiply(b, h)
-
         gather(xwg, xw[:].bitcast(U32), 0, S)
         gather(xsg, xs[:], 0, S)
         round_filter("s", "r", 0)
         round_filter("s", "i", 0)
         negate("s", 0)
-        quantise(0)
-        gather(esg, es[:], 0, S)
-        quantise_minus(0)
-        multiply_part(0, 0, 0)
-        gather(ewg, ew[:].bitcast(U32), 0, HALF)
-        multiply_part(0, 0, 1)
-        multiply_part(0, 1, 0)
-        gather(ewg, ew[:].bitcast(U32), HALF, S)
-        multiply_part(0, 1, 1)
+        quantise(0, 1, 2)
+        gather(ewg, ew[:].bitcast(U32), 0, S)
+        quantise(0, 0, 1)
+        filters_stationary(0, 0, 0)
+        gather(esg, es[:], 0, HALF)
+        filters_stationary(0, 0, 1)
+        filters_stationary(0, 1, 0)
+        gather(esg, es[:], HALF, S)
+        filters_stationary(0, 1, 1)
         round_filter("s", "r", 1)
-        round_filter("v", "i", 1)
-        quantise(1)
+        round_filter("s", "i", 1)
         negate("v", 1)
-        quantise_minus(1)
-        multiply(1, 0)
-        multiply(1, 1)
-        square(0, 0)
-        make_power(0, 0, HALF)
-        make_pairs(0, 0, HALF)
+        quantise(1, 1, 2)
+        quantise(1, 0, 1)
         round_filter("s", "r", 2)
-        round_filter("v", "i", 2)
-        quantise(2)
+        round_filter("s", "i", 2)
         negate("v", 2)
-        quantise_minus(2)
-        multiply(2, 0)
-        multiply(2, 1)
-        square(0, 1)
-        make_power(0, HALF, S)
-        make_noise(0, 0, HALF)
-        make_inverse(0, 0, HALF)
-        make_pairs(0, HALF, S)
-        make_inverse2(0, 0, HALF)
-        round_filter("s", "r", 3)
+        quantise(2, 1, 2)
+        quantise(2, 0, 1)
+        square_rows(0, 0)
+        square_rows(0, 1)
+        add_rows(0, 0, S)
+        bins_stationary(1, 0, 0)
+        bins_stationary(1, 0, 1)
+        bins_stationary(1, 1, 0)
+        bins_stationary(1, 1, 1)
+        round_filter("v", "r", 3)
         round_filter("v", "i", 3)
-        quantise(3)
+        make_pairs(0, 0, S)
         negate("v", 3)
-        quantise_minus(3)
-        multiply(3, 0)
-        multiply(3, 1)
-        square(1, 0)
-        square(1, 1)
-        make_power(1, 0, S)
-        make_noise(0, HALF, S)
-        make_inverse(0, HALF, S)
-        make_pairs(1, 0, S)
-        make_inverse2(0, HALF, S)
-        square(2, 0)
-        square(2, 1)
-        make_power(2, 0, S)
-        make_noise(1, 0, S)
-        make_inverse(1, 0, S)
+        quantise(3, 1, 2)
+        quantise(3, 0, 1)
+        square_bins(1, 0)
+        square_bins(1, 1)
+        filters_stationary(2, 0, 0)
+        filters_stationary(2, 0, 1)
+        filters_stationary(2, 1, 0)
+        filters_stationary(2, 1, 1)
+        root_rows(0, 0, S)
+        turn_low(1, unsummed(1))
+        square_rows(2, 0)
+        square_rows(2, 1)
+        make_least(0, 0, S)
+        filters_stationary(3, 0, 0)
+        filters_stationary(3, 0, 1)
+        filters_stationary(3, 1, 0)
+        filters_stationary(3, 1, 1)
+        add_rows(2, 0, S)
+        make_inverse(0, 0, S)
+        root_low(1)
+        turn_high(1, unsummed(1))
+        turn_power(1, unsummed(1))
         make_pairs(2, 0, S)
-        make_inverse2(1, 0, S)
-        make_ratio(0, 0, HALF)
-        square(3, 0)
-        make_power(3, 0, HALF)
-        make_noise(2, 0, S)
-        make_inverse(2, 0, S)
+        square_rows(3, 0)
+        make_ratio(0, 0, S)
+        square_rows(3, 1)
+        root_rows(2, 0, S)
+        root_high(1)
+        add_rows(3, 0, HALF)
+        finish("s", 0, 0, S)
         make_pairs(3, 0, HALF)
-        make_inverse2(2, 0, S)
-        make_ratio(0, HALF, S)
-        finish("s", 0, 0, HALF)
-        square(3, 1)
-        make_power(3, HALF, S)
-        make_noise(3, 0, HALF)
-        make_inverse(3, 0, HALF)
+        make_least(2, 0, S)
+        make_least(1, 0, S)
+        add_rows(3, HALF, S)
+        root_rows(3, 0, HALF)
+        make_inverse(2, 0, S)
         make_pairs(3, HALF, S)
-        make_inverse2(3, 0, HALF)
-        make_ratio(1, 0, S)
-        finish("s", 0, HALF, S)
-        make_noise(3, HALF, S)
-        make_inverse(3, HALF, S)
-        make_inverse2(3, HALF, S)
+        make_inverse(1, 0, S)
+        root_rows(3, HALF, S)
+        make_least(3, 0, HALF)
         make_ratio(2, 0, S)
-        finish("s", 1, 0, S)
-        make_ratio(3, 0, HALF)
+        make_least(3, HALF, S)
+        make_ratio(1, 0, S)
+        make_inverse(3, 0, HALF)
         finish("v", 2, 0, S)
+        make_inverse(3, HALF, S)
+        finish("v", 1, 0, S)
+        make_ratio(3, 0, HALF)
         make_ratio(3, HALF, S)
         finish("v", 3, 0, HALF)
         finish("v", 3, HALF, S)

@@ -273,28 +273,28 @@ def tile_picked_ycfar_go_p_kernel(
         turn_power(1, unsummed(1))
         make_pairs(2, 0, S)
         square_rows(3, 0)
-        make_ratio(0, 0, S)
         square_rows(3, 1)
         root_rows(2, 0, S)
-        root_high(1)
         add_rows(3, 0, HALF)
-        finish("s", 0, 0, S)
+        add_rows(3, HALF, S)
         make_pairs(3, 0, HALF)
+        make_pairs(3, HALF, S)
+        make_ratio(0, 0, S)
+        root_high(1)
+        root_rows(3, 0, HALF)
+        root_rows(3, HALF, S)
         make_least(2, 0, S)
         make_least(1, 0, S)
-        add_rows(3, HALF, S)
-        root_rows(3, 0, HALF)
         make_inverse(2, 0, S)
-        make_pairs(3, HALF, S)
         make_inverse(1, 0, S)
-        root_rows(3, HALF, S)
         make_least(3, 0, HALF)
-        make_ratio(2, 0, S)
         make_least(3, HALF, S)
-        make_ratio(1, 0, S)
+        finish("s", 0, 0, S)
         make_inverse(3, 0, HALF)
-        finish("v", 2, 0, S)
         make_inverse(3, HALF, S)
+        make_ratio(2, 0, S)
+        make_ratio(1, 0, S)
+        finish("s", 2, 0, S)
         finish("v", 1, 0, S)
         make_ratio(3, 0, HALF)
         make_ratio(3, HALF, S)

@@ -21,8 +21,10 @@ PACK = 4
 BANDS = V // P
 HALF = S // 2
 PAD = 4
-SHARES = {"squares0":"raw_r2"}
-BANKS = {"product0_0":0,"product0_1":1,"product1_0":2,"product1_1":3,"product2_0":4,"product2_1":5,"product3_0":0,"product3_1":1,"low1":6,"high1":7,"power1":2}
+FIRST, TURNED, MIDDLE, LAST = range(BANDS)
+PRODUCT_BANKS = 6
+WHOLE = ((0, S),)
+HALVES = ((0, HALF), (HALF, S))
 
 
 def tile_picked_ycfar_go_p_kernel(
@@ -33,11 +35,14 @@ def tile_picked_ycfar_go_p_kernel(
         keep = ctx.enter_context(tc.tile_pool(name="keep", bufs=1))
         psum = ctx.enter_context(tc.psum_pool(name="psum", bufs=1))
 
-        def sbuf(name, shape, dtype):
-            return keep.tile(shape, dtype, name=name, tag=SHARES.get(name, name), align_bytes=64)
+        def sbuf(name, shape, dtype, over=None):
+            return keep.tile(shape, dtype, name=name, tag=over or name, align_bytes=64)
 
-        def bank(name):
-            return psum.tile([P, S], F32, name=name, tag="bank%d" % BANKS[name])
+        def bank(name, number):
+            return psum.tile([P, S], F32, name=name, tag="bank%d" % number)
+
+        def per_band(name, shape, dtype):
+            return [sbuf("%s%d" % (name, b), shape, dtype) for b in range(BANDS)]
 
         offsets = keep.tile([P, S // 16], U16, name="offsets")
         xw, ew = sbuf("xw", [P, T], I32), sbuf("ew", [P, T], I32)
@@ -47,13 +52,13 @@ def tile_picked_ycfar_go_p_kernel(
         ones = sbuf("ones", [P, BANDS, PAD], F32)
         root = sbuf("root", [P, BANDS, PAD + S], F32)
         ident = sbuf("ident", [P, P], F32)
-        power = [sbuf("power%d" % b, [P, PAD + S], F32) for b in range(BANDS)]
+        power = {b: sbuf("power%d" % b, [P, PAD + S], F32) for b in range(BANDS) if b != TURNED}
 
         nc.vector.memset(xs[:].bitcast(I32), 0)
         nc.vector.memset(ones[:], 1.0)
         nc.vector.memset(es[:].bitcast(I32), 0)
-        for b in (0, 2, 3):
-            nc.vector.memset(power[b][:, 0:PAD], 0.0)
+        for tile in power.values():
+            nc.vector.memset(tile[:, 0:PAD], 0.0)
         make_identity(nc, ident[:])
 
         def load_words(tile, words):
@@ -65,28 +70,24 @@ def tile_picked_ycfar_go_p_kernel(
 
         raw = {}
 
-        def load_filter(name, h, b):
-            raw[name, b] = sbuf("raw_%s%d" % (name, b), [P, PACK, P], F32)
-            nc.sync.dma_start(raw[name, b][:], h[:, b * P : (b + 1) * P].rearrange("(p j) w -> p j w", j=PACK))
+        def load_filters(b):
+            for name, h in (("r", hr), ("i", hi)):
+                raw[name, b] = sbuf("raw_%s%d" % (name, b), [P, PACK, P], F32)
+                nc.sync.dma_start(raw[name, b][:], h[:, b * P : (b + 1) * P].rearrange("(p j) w -> p j w", j=PACK))
 
         nc.sync.dma_start(offsets[:], offs)
         nc.scalar.activation(root[:, :, 0:PAD], ones[:], ACT.Abs_reciprocal_sqrt, scale=0.2)
         load_words(xw, x_words)
         load_scales(xs, x_scales)
-        load_filter("r", hr, 0)
-        load_filter("i", hi, 0)
+        load_filters(FIRST)
         load_words(ew, e_words)
         load_scales(es, e_scales)
-        load_filter("r", hr, 1)
-        load_filter("i", hi, 1)
-        load_filter("r", hr, 2)
-        load_filter("i", hi, 2)
-        load_filter("r", hr, 3)
-        load_filter("i", hi, 3)
+        for b in range(FIRST + 1, BANDS):
+            load_filters(b)
 
-        rounded = [sbuf("rounded%d" % b, [P, 3, P * PACK], BF16) for b in range(BANDS)]
-        words = [sbuf("words%d" % b, [P, 3 * P], U32) for b in range(BANDS)]
-        planes = [sbuf("planes%d" % b, [P, 3 * P], U8) for b in range(BANDS)]
+        rounded = per_band("rounded", [P, 3, P * PACK], BF16)
+        words = per_band("words", [P, 3 * P], U32)
+        planes = per_band("planes", [P, 3 * P], U8)
 
         def interleaved(tile):
             return tile.rearrange("p (c i t) -> p c t i", i=4, t=PACK)
@@ -94,209 +95,186 @@ def tile_picked_ycfar_go_p_kernel(
         def rows(name, b):
             return raw[name, b][:].rearrange("p t (c i) -> p c t i", i=4)
 
-        def round_filter(engine, name, b):
-            copy = nc.vector.tensor_copy if engine == "v" else nc.scalar.copy
-            copy(interleaved(rounded[b][:, "mri".index(name), :]), rows(name, b))
+        def round_filters(b):
+            copy = nc.vector.tensor_copy if b == LAST else nc.scalar.copy
+            for place, name in ((1, "r"), (2, "i")):
+                copy(interleaved(rounded[b][:, place, :]), rows(name, b))
 
-        def negate(engine, b):
-            if engine == "v":
-                nc.vector.tensor_scalar(rounded[b][:, 0, :], rounded[b][:, 2, :], -1.0, None, ALU.mult)
-            else:
+        def negate(b):
+            if b == FIRST:
                 nc.scalar.activation(interleaved(rounded[b][:, 0, :]), rows("i", b), ACT.Copy, scale=-1.0)
+            else:
+                nc.vector.tensor_scalar(rounded[b][:, 0, :], rounded[b][:, 2, :], -1.0, None, ALU.mult)
 
         def quantise(b, first, count):
             cols = slice(first * P, (first + count) * P)
-            nc.vector.quantize_mx(words[b][:, cols].bitcast(FP8X4), planes[b][:, cols], rounded[b][:, first : first + count, :].rearrange("p n w -> p (n w)"))
+            nc.vector.quantize_mx(
+                words[b][:, cols].bitcast(FP8X4), planes[b][:, cols],
+                rounded[b][:, first : first + count, :].rearrange("p n w -> p (n w)"),
+            )
+
+        def quantise_band(b):
+            negate(b)
+            quantise(b, 1, 2)
+            quantise(b, 0, 1)
 
         def gather(picked, window, lo, up):
             nc.vector.tensor_copy(picked[:, lo:up], window.indirect(offsets[:, lo // 16 : up // 16]))
 
-        squares = [sbuf("squares%d" % b, [P, 2 * S], F32) for b in range(BANDS)]
-        pairs = [sbuf("pairs%d" % b, [P, S], F32) for b in range(BANDS)]
-        least = [sbuf("least%d" % b, [P, S], F32) for b in range(BANDS)]
-        inv = [sbuf("inv%d" % b, [P, S], F32) for b in range(BANDS)]
-        ratio = [sbuf("ratio%d" % b, [P, S], F32) for b in range(BANDS)]
-        res = [sbuf("res%d" % b, [P, S], F32) for b in range(BANDS)]
+        squares = [sbuf("squares%d" % b, [P, 2 * S], F32, "raw_r%d" % MIDDLE if b == FIRST else None) for b in range(BANDS)]
+        pairs = {b: sbuf("pairs%d" % b, [P, S], F32) for b in power}
+        least = per_band("least", [P, S], F32)
+        inverse = per_band("inverse", [P, S], F32)
+        ratio = per_band("ratio", [P, S], F32)
+        result = per_band("result", [P, S], F32)
         picked = ((xwg, xsg), (ewg, esg))
-        held = {}
+        product, turned = {}, {}
 
-        def filters_stationary(b, h, table):
+        def multiply(b, h, table):
             if table == 0:
-                held["product", b, h] = bank("product%d_%d" % (b, h))
-            cols = slice(h * HALF, (h + 1) * HALF)
-            for part in range(2):
-                mine = slice((1 - table + part) * P, (2 - table + part) * P)
+                product[b, h] = bank("product%d_%d" % (b, h), (2 * b + h) % PRODUCT_BANKS)
+            for n in range(2):
+                if b == TURNED:
+                    filters = slice((1 - table) * P, (3 - table) * P)
+                    bins = slice((2 * h + n) * P, (2 * h + n + 1) * P)
+                else:
+                    filters = slice((1 - table + n) * P, (2 - table + n) * P)
+                    bins = slice(h * HALF, (h + 1) * HALF)
+                own = (words[b][:, filters].bitcast(FP8X4), planes[b][:, filters])
+                looked_up = (picked[table][0][:, bins].bitcast(FP8X4), picked[table][1][:, bins])
+                still, moving = (looked_up, own) if b == TURNED else (own, looked_up)
                 nc.tensor.matmul_mx(
-                    held["product", b, h][:, part * HALF : (part + 1) * HALF],
-                    lhsT=words[b][:, mine].bitcast(FP8X4), lhsT_scale=planes[b][:, mine],
-                    rhs=picked[table][0][:, cols].bitcast(FP8X4), rhs_scale=picked[table][1][:, cols],
-                    start=(table, part) == (0, 0), stop=(table, part) == (1, 1),
+                    product[b, h][:, n * HALF : (n + 1) * HALF],
+                    lhsT=still[0], lhsT_scale=still[1], rhs=moving[0], rhs_scale=moving[1],
+                    start=(table, n) == (0, 0), stop=(table, n) == (1, 1),
                 )
 
-        def bins_stationary(b, h, table):
-            if table == 0:
-                held["product", b, h] = bank("product%d_%d" % (b, h))
-            mine = slice((1 - table) * P, (3 - table) * P)
-            for block in range(2):
-                cols = slice((2 * h + block) * P, (2 * h + block + 1) * P)
-                nc.tensor.matmul_mx(
-                    held["product", b, h][:, block * 2 * P : (block + 1) * 2 * P],
-                    lhsT=picked[table][0][:, cols].bitcast(FP8X4), lhsT_scale=picked[table][1][:, cols],
-                    rhs=words[b][:, mine].bitcast(FP8X4), rhs_scale=planes[b][:, mine],
-                    start=(table, block) == (0, 0), stop=(table, block) == (1, 1),
+        def multiply_band(b):
+            for h in range(2):
+                for table in range(2):
+                    multiply(b, h, table)
+
+        def square(b):
+            for h in range(2):
+                if b == TURNED:
+                    nc.scalar.activation(squares[b][:, h * S : (h + 1) * S], product[b, h][:], ACT.Square)
+                else:
+                    target = squares[b][:].rearrange("p (part s) -> p part s", part=2)[:, :, h * HALF : (h + 1) * HALF]
+                    nc.scalar.activation(target, product[b, h][:].rearrange("p (part s) -> p part s", part=2), ACT.Square)
+
+        def turn(name, number, passes):
+            turned[name] = bank(name, number)
+            sources = [(2 * block + part, column) for block, column in passes for part in range(2)]
+            for n, (piece, column) in enumerate(sources):
+                nc.tensor.matmul(
+                    turned[name][:, column : column + P], squares[TURNED][:, piece * P : (piece + 1) * P], ident[:],
+                    start=n == 0, stop=n == len(sources) - 1, is_transpose=True,
                 )
 
-        def square_rows(b, h):
-            target = squares[b][:].rearrange("p (part s) -> p part s", part=2)[:, :, h * HALF : (h + 1) * HALF]
-            nc.scalar.activation(target, held["product", b, h][:].rearrange("p (part s) -> p part s", part=2), ACT.Square)
+        def turn_low():
+            turn("low", PRODUCT_BANKS, [(block, block * P) for block in range(3)] + [(block, block * P + 1) for block in range(2)])
 
-        def square_bins(b, h):
-            nc.scalar.activation(squares[b][:, h * S : (h + 1) * S], held["product", b, h][:], ACT.Square)
+        def turn_high():
+            turn("high", PRODUCT_BANKS + 1, [(block, (block - 1) * P) for block in range(1, 4)] + [(block, (block - 1) * P - 1) for block in range(2, 4)])
 
-        def add_rows(b, lo, up):
-            nc.vector.tensor_tensor(power[b][:, PAD + lo : PAD + up], squares[b][:, lo:up], squares[b][:, S + lo : S + up], ALU.add)
+        def turn_power():
+            turn("power", 2 * TURNED, [(block, block * P) for block in range(4)])
 
-        def add_bins(b):
-            parts = squares[b][:].rearrange("p (block part t) -> p block part t", part=2, t=P)
-            nc.vector.tensor_tensor(power[b][:, 0:S].rearrange("p (block t) -> p block t", t=P), parts[:, :, 0, :], parts[:, :, 1, :], ALU.add)
+        def inverse_root(b, lo, up, sums):
+            nc.scalar.activation(root[:, b, PAD + lo : PAD + up], sums, ACT.Abs_reciprocal_sqrt, bias=0.2, scale=0.5)
 
-        def turn(name, b, passes, sources):
-            held[name, b] = bank("%s%d" % (name, b))
-            total = len(passes) * len(sources)
-            for n, (block, column) in enumerate(passes):
-                for k, source in enumerate(sources):
-                    nc.tensor.matmul(
-                        held[name, b][:, column : column + P], source(block), ident[:],
-                        start=n * len(sources) + k == 0, stop=n * len(sources) + k == total - 1, is_transpose=True,
-                    )
+        def parts(b):
+            return HALVES if b == LAST else WHOLE
 
-        def summed(b):
-            return [lambda block: power[b][:, block * P : (block + 1) * P]]
+        def add_squares(b):
+            for lo, up in parts(b):
+                nc.vector.tensor_tensor(power[b][:, PAD + lo : PAD + up], squares[b][:, lo:up], squares[b][:, S + lo : S + up], ALU.add)
 
-        def unsummed(b):
-            return [lambda block, part=part: squares[b][:, (2 * block + part) * P : (2 * block + part + 1) * P] for part in range(2)]
+        def add_pairs(b):
+            for lo, up in parts(b):
+                nc.vector.tensor_tensor(pairs[b][:, lo:up], power[b][:, PAD + lo : PAD + up], power[b][:, PAD - 1 + lo : PAD - 1 + up], ALU.add)
 
-        def turn_power(b, sources):
-            turn("power", b, [(block, block * P) for block in range(4)], sources)
+        def take_roots(b):
+            for lo, up in parts(b):
+                inverse_root(b, lo, up, pairs[b][:, lo:up])
 
-        def turn_low(b, sources):
-            turn("low", b, [(block, block * P) for block in range(3)] + [(block, block * P + 1) for block in range(2)], sources)
+        def take_least(b):
+            for lo, up in parts(b):
+                nc.vector.tensor_tensor(least[b][:, lo:up], root[:, b, PAD - 2 + lo : PAD - 2 + up], root[:, b, PAD - 4 + lo : PAD - 4 + up], ALU.min)
 
-        def turn_high(b, sources):
-            turn("high", b, [(block, (block - 1) * P) for block in (1, 2, 3)] + [(block, (block - 1) * P - 1) for block in (2, 3)], sources)
+        def invert(b):
+            for lo, up in parts(b):
+                nc.scalar.activation(inverse[b][:, lo:up], least[b][:, lo:up], ACT.Square)
 
-        def root_low(b):
-            nc.scalar.activation(root[:, b, PAD : PAD + HALF], held["low", b][:, 0:HALF], ACT.Abs_reciprocal_sqrt, bias=0.2, scale=0.5)
+        def divide(b):
+            for lo, up in parts(b):
+                source = turned["power"][:, lo:up] if b == TURNED else power[b][:, PAD + lo : PAD + up]
+                nc.vector.tensor_tensor(ratio[b][:, lo:up], source, inverse[b][:, lo:up], ALU.mult)
 
-        def root_high(b):
-            nc.scalar.activation(root[:, b, PAD + HALF : PAD + S - 2], held["high", b][:, P - 1 : P - 1 + HALF - 2], ACT.Abs_reciprocal_sqrt, bias=0.2, scale=0.5)
+        def finish(b):
+            for lo, up in parts(b):
+                if b % 2:
+                    nc.vector.tensor_scalar(result[b][:, lo:up], ratio[b][:, lo:up], -1.0, 0.0, ALU.add, ALU.max)
+                else:
+                    nc.scalar.activation(result[b][:, lo:up], ratio[b][:, lo:up], ACT.Relu, bias=-1.0)
+                nc.sync.dma_start(out[b * P : (b + 1) * P, lo:up], result[b][:, lo:up])
 
-        def make_pairs(b, lo, up):
-            nc.vector.tensor_tensor(pairs[b][:, lo:up], power[b][:, PAD + lo : PAD + up], power[b][:, PAD - 1 + lo : PAD - 1 + up], ALU.add)
+        def roots_low():
+            inverse_root(TURNED, 0, HALF, turned["low"][:, 0:HALF])
 
-        def root_rows(b, lo, up):
-            nc.scalar.activation(root[:, b, PAD + lo : PAD + up], pairs[b][:, lo:up], ACT.Abs_reciprocal_sqrt, bias=0.2, scale=0.5)
-
-        def make_least(b, lo, up):
-            nc.vector.tensor_tensor(least[b][:, lo:up], root[:, b, PAD - 2 + lo : PAD - 2 + up], root[:, b, PAD - 4 + lo : PAD - 4 + up], ALU.min)
-
-        def make_inverse(b, lo, up):
-            nc.scalar.activation(inv[b][:, lo:up], least[b][:, lo:up], ACT.Square)
-
-        def make_ratio(b, lo, up):
-            source = held["power", b][:, lo:up] if ("power", b) in held else power[b][:, PAD + lo : PAD + up]
-            nc.vector.tensor_tensor(ratio[b][:, lo:up], source, inv[b][:, lo:up], ALU.mult)
-
-        def finish(engine, b, lo, up):
-            if engine == "v":
-                nc.vector.tensor_scalar(res[b][:, lo:up], ratio[b][:, lo:up], -1.0, 0.0, ALU.add, ALU.max)
-            else:
-                nc.scalar.activation(res[b][:, lo:up], ratio[b][:, lo:up], ACT.Relu, bias=-1.0)
-            nc.sync.dma_start(out[b * P : (b + 1) * P, lo:up], res[b][:, lo:up])
+        def roots_high():
+            inverse_root(TURNED, HALF, S - 2, turned["high"][:, P - 1 : P - 1 + HALF - 2])
 
         gather(xwg, xw[:].bitcast(U32), 0, S)
         gather(xsg, xs[:], 0, S)
-        round_filter("s", "r", 0)
-        round_filter("s", "i", 0)
-        negate("s", 0)
-        quantise(0, 1, 2)
+        round_filters(FIRST)
+        negate(FIRST)
+        quantise(FIRST, 1, 2)
         gather(ewg, ew[:].bitcast(U32), 0, S)
-        quantise(0, 0, 1)
-        filters_stationary(0, 0, 0)
-        gather(esg, es[:], 0, HALF)
-        filters_stationary(0, 0, 1)
-        filters_stationary(0, 1, 0)
-        gather(esg, es[:], HALF, S)
-        filters_stationary(0, 1, 1)
-        round_filter("s", "r", 1)
-        round_filter("s", "i", 1)
-        negate("v", 1)
-        quantise(1, 1, 2)
-        quantise(1, 0, 1)
-        round_filter("s", "r", 2)
-        round_filter("s", "i", 2)
-        negate("v", 2)
-        quantise(2, 1, 2)
-        quantise(2, 0, 1)
-        square_rows(0, 0)
-        square_rows(0, 1)
-        add_rows(0, 0, S)
-        bins_stationary(1, 0, 0)
-        bins_stationary(1, 0, 1)
-        bins_stationary(1, 1, 0)
-        bins_stationary(1, 1, 1)
-        round_filter("v", "r", 3)
-        round_filter("v", "i", 3)
-        make_pairs(0, 0, S)
-        negate("v", 3)
-        quantise(3, 1, 2)
-        quantise(3, 0, 1)
-        square_bins(1, 0)
-        square_bins(1, 1)
-        filters_stationary(2, 0, 0)
-        filters_stationary(2, 0, 1)
-        filters_stationary(2, 1, 0)
-        filters_stationary(2, 1, 1)
-        root_rows(0, 0, S)
-        turn_low(1, unsummed(1))
-        square_rows(2, 0)
-        square_rows(2, 1)
-        make_least(0, 0, S)
-        filters_stationary(3, 0, 0)
-        filters_stationary(3, 0, 1)
-        filters_stationary(3, 1, 0)
-        filters_stationary(3, 1, 1)
-        add_rows(2, 0, S)
-        make_inverse(0, 0, S)
-        root_low(1)
-        turn_high(1, unsummed(1))
-        turn_power(1, unsummed(1))
-        make_pairs(2, 0, S)
-        square_rows(3, 0)
-        square_rows(3, 1)
-        root_rows(2, 0, S)
-        add_rows(3, 0, HALF)
-        add_rows(3, HALF, S)
-        make_pairs(3, 0, HALF)
-        make_pairs(3, HALF, S)
-        make_ratio(0, 0, S)
-        root_high(1)
-        root_rows(3, 0, HALF)
-        root_rows(3, HALF, S)
-        make_least(2, 0, S)
-        make_least(1, 0, S)
-        make_inverse(2, 0, S)
-        make_inverse(1, 0, S)
-        make_least(3, 0, HALF)
-        make_least(3, HALF, S)
-        finish("s", 0, 0, S)
-        make_inverse(3, 0, HALF)
-        make_inverse(3, HALF, S)
-        make_ratio(2, 0, S)
-        make_ratio(1, 0, S)
-        finish("s", 2, 0, S)
-        finish("v", 1, 0, S)
-        make_ratio(3, 0, HALF)
-        make_ratio(3, HALF, S)
-        finish("v", 3, 0, HALF)
-        finish("v", 3, HALF, S)
+        quantise(FIRST, 0, 1)
+        for h, (lo, up) in enumerate(HALVES):
+            multiply(FIRST, h, 0)
+            gather(esg, es[:], lo, up)
+            multiply(FIRST, h, 1)
+        for b in (TURNED, MIDDLE):
+            round_filters(b)
+            quantise_band(b)
+
+        square(FIRST)
+        add_squares(FIRST)
+        multiply_band(TURNED)
+        round_filters(LAST)
+        quantise_band(LAST)
+        add_pairs(FIRST)
+        square(TURNED)
+        multiply_band(MIDDLE)
+        take_roots(FIRST)
+        square(MIDDLE)
+        multiply_band(LAST)
+        turn_low()
+        take_least(FIRST)
+        add_squares(MIDDLE)
+        invert(FIRST)
+        turn_high()
+        turn_power()
+        add_pairs(MIDDLE)
+        square(LAST)
+        take_roots(MIDDLE)
+        add_squares(LAST)
+        add_pairs(LAST)
+        take_least(MIDDLE)
+        divide(FIRST)
+        take_roots(LAST)
+        roots_low()
+        roots_high()
+        invert(MIDDLE)
+        take_least(TURNED)
+        invert(TURNED)
+        finish(FIRST)
+        divide(MIDDLE)
+        take_least(LAST)
+        finish(MIDDLE)
+        invert(LAST)
+        for b in (TURNED, LAST):
+            divide(b)
+            finish(b)

@@ -65,8 +65,8 @@ def tile_picked_ycfar_go_p_kernel(
             nc.sync.dma_start(tile[:], words[0].rearrange("p n t -> p (n t)").bitcast(I32))
 
         def load_scales(tile, scales):
-            for q in range(4):
-                nc.sync.dma_start(tile[32 * q : 32 * q + 4, :].bitcast(I32), scales[0, 4 * q : 4 * q + 4, :].bitcast(I32))
+            for r in range(4):
+                nc.sync.dma_start(tile[r:P:32, :].bitcast(I32), scales[0, r:16:4, :].bitcast(I32))
 
         raw = {}
 

@@ -119,7 +119,8 @@ def tile_picked_ycfar_go_p_kernel(
             quantise(b, 0, 1)
 
         def gather(picked, window, lo, up):
-            nc.vector.tensor_copy(picked[:, lo:up], window.indirect(offsets[:, lo // 16 : up // 16]))
+            dealt = picked[:, lo:up].rearrange("p (h s i) -> p h i s", s=2, i=P)
+            nc.vector.tensor_copy(dealt, window.indirect(offsets[:, lo // 16 : up // 16]))
 
         squares = [sbuf("squares%d" % b, [P, 2 * S], F32, "raw_r%d" % MIDDLE if b == FIRST else None) for b in range(BANDS)]
         pairs = {b: sbuf("pairs%d" % b, [P, S], F32) for b in power}
@@ -160,7 +161,8 @@ def tile_picked_ycfar_go_p_kernel(
                     nc.scalar.activation(squares[b][:, h * S : (h + 1) * S], product[b, h][:], ACT.Square)
                 else:
                     target = squares[b][:].rearrange("p (part s) -> p part s", part=2)[:, :, h * HALF : (h + 1) * HALF]
-                    nc.scalar.activation(target, product[b, h][:].rearrange("p (part s) -> p part s", part=2), ACT.Square)
+                    source = product[b, h][:].rearrange("p (part s i) -> p part i s", part=2, s=2)
+                    nc.scalar.activation(target.rearrange("p part (i s) -> p part i s", s=2), source, ACT.Square)
 
         def turn(name, number, passes):
             turned[name] = bank(name, number)
@@ -171,14 +173,15 @@ def tile_picked_ycfar_go_p_kernel(
                     start=n == 0, stop=n == len(sources) - 1, is_transpose=True,
                 )
 
-        def turn_low():
-            turn("low", PRODUCT_BANKS, [(block, block * P) for block in range(3)] + [(block, block * P + 1) for block in range(2)])
-
-        def turn_high():
-            turn("high", PRODUCT_BANKS + 1, [(block, (block - 1) * P) for block in range(1, 4)] + [(block, (block - 1) * P - 1) for block in range(2, 4)])
+        def turn_pairs():
+            aligned = [(2 * h + s, h * P + up) for h in range(2) for s, up in ((0, 0), (1, 0), (1, HALF))]
+            turn("pairs", PRODUCT_BANKS, aligned + [(2 * h, HALF + h * P - 1) for h in range(2)])
 
         def turn_power():
-            turn("power", 2 * TURNED, [(block, block * P) for block in range(4)])
+            turn("power", PRODUCT_BANKS + 1, [(2 * h + s, s * HALF + h * P) for h in range(2) for s in range(2)])
+
+        def in_list_order(tile):
+            return tile.rearrange("p (s n) -> p n s", s=2)
 
         def inverse_root(b, lo, up, sums):
             nc.scalar.activation(root[:, b, PAD + lo : PAD + up], sums, ACT.Abs_reciprocal_sqrt, bias=0.2, scale=0.5)
@@ -208,8 +211,11 @@ def tile_picked_ycfar_go_p_kernel(
 
         def divide(b):
             for lo, up in parts(b):
-                source = turned["power"][:, lo:up] if b == TURNED else power[b][:, PAD + lo : PAD + up]
-                nc.vector.tensor_tensor(ratio[b][:, lo:up], source, inverse[b][:, lo:up], ALU.mult)
+                if b == TURNED:
+                    paired = [t[b][:].rearrange("p (n s) -> p n s", s=2) for t in (ratio, inverse)]
+                    nc.vector.tensor_tensor(paired[0], in_list_order(turned["power"][:]), paired[1], ALU.mult)
+                else:
+                    nc.vector.tensor_tensor(ratio[b][:, lo:up], power[b][:, PAD + lo : PAD + up], inverse[b][:, lo:up], ALU.mult)
 
         def finish(b):
             for lo, up in parts(b):
@@ -219,11 +225,10 @@ def tile_picked_ycfar_go_p_kernel(
                     nc.scalar.activation(result[b][:, lo:up], ratio[b][:, lo:up], ACT.Relu, bias=-1.0)
                 nc.sync.dma_start(out[b * P : (b + 1) * P, lo:up], result[b][:, lo:up])
 
-        def roots_low():
-            inverse_root(TURNED, 0, HALF, turned["low"][:, 0:HALF])
-
-        def roots_high():
-            inverse_root(TURNED, HALF, S - 2, turned["high"][:, P - 1 : P - 1 + HALF - 2])
+        def turned_roots():
+            target = root[:, TURNED, PAD + 1 : PAD + S - 1].rearrange("p (n s) -> p n s", s=2)
+            nc.scalar.activation(target, in_list_order(turned["pairs"][:])[:, 0 : HALF - 1, :], ACT.Abs_reciprocal_sqrt, bias=0.2, scale=0.5)
+            inverse_root(TURNED, 0, 1, turned["power"][:, 0:1])
 
         gather(xwg, xw[:].bitcast(U32), 0, S)
         gather(xsg, xs[:], 0, S)
@@ -251,11 +256,10 @@ def tile_picked_ycfar_go_p_kernel(
         take_roots(FIRST)
         square(MIDDLE)
         multiply_band(LAST)
-        turn_low()
+        turn_pairs()
         take_least(FIRST)
         add_squares(MIDDLE)
         invert(FIRST)
-        turn_high()
         turn_power()
         add_pairs(MIDDLE)
         square(LAST)
@@ -265,8 +269,7 @@ def tile_picked_ycfar_go_p_kernel(
         take_least(MIDDLE)
         divide(FIRST)
         take_roots(LAST)
-        roots_low()
-        roots_high()
+        turned_roots()
         invert(MIDDLE)
         take_least(TURNED)
         invert(TURNED)

@@ -21,10 +21,14 @@ PACK = 4
 BANDS = V // P
 HALF = S // 2
 PAD = 4
-FIRST, TURNED, MIDDLE, LAST = range(BANDS)
-PRODUCT_BANKS = 6
-WHOLE = ((0, S),)
+A, B, C, D = range(BANDS)
+TURNED = (B, C, D)
+SUMMED = (B, C, D)
+WHOLE = (0, S)
 HALVES = ((0, HALF), (HALF, S))
+PRODUCT_BANKS = {A: 0, B: 2, C: 4, D: 0}
+PAIR_BANK = {B: 6, C: 2, D: 4}
+POWER_BANK = {B: 7, C: 3, D: 5}
 
 
 def tile_picked_ycfar_go_p_kernel(
@@ -41,8 +45,8 @@ def tile_picked_ycfar_go_p_kernel(
         def bank(name, number):
             return psum.tile([P, S], F32, name=name, tag="bank%d" % number)
 
-        def per_band(name, shape, dtype):
-            return [sbuf("%s%d" % (name, b), shape, dtype) for b in range(BANDS)]
+        def per_band(name, shape, dtype, over=None):
+            return [sbuf("%s%d" % (name, b), shape, dtype, (over or {}).get(b)) for b in range(BANDS)]
 
         offsets = keep.tile([P, S // 16], U16, name="offsets")
         xw, ew = sbuf("xw", [P, T], I32), sbuf("ew", [P, T], I32)
@@ -50,234 +54,303 @@ def tile_picked_ycfar_go_p_kernel(
         xwg, ewg = sbuf("xwg", [P, S], U32), sbuf("ewg", [P, S], U32)
         xsg, esg = sbuf("xsg", [P, S], U8), sbuf("esg", [P, S], U8)
         ones = sbuf("ones", [P, BANDS, PAD], F32)
-        root = sbuf("root", [P, BANDS, PAD + S], F32)
+        root = sbuf("root", [P, BANDS, PAD + S + PAD], F32)
         ident = sbuf("ident", [P, P], F32)
-        power = {b: sbuf("power%d" % b, [P, PAD + S], F32) for b in range(BANDS) if b != TURNED}
+        power = sbuf("power", [P, PAD + S], F32)
+        twice = sbuf("twice", [P, PAD + S], F32)
 
         nc.vector.memset(xs[:].bitcast(I32), 0)
         nc.vector.memset(ones[:], 1.0)
         nc.vector.memset(es[:].bitcast(I32), 0)
-        for tile in power.values():
-            nc.vector.memset(tile[:, 0:PAD], 0.0)
+        nc.vector.memset(power[:, 0:PAD], 0.0)
+        nc.vector.tensor_scalar(twice[:, 0:PAD], ones[:, 0, :], 0.4, None, ALU.mult)
         make_identity(nc, ident[:])
 
         def load_words(tile, words):
             nc.sync.dma_start(tile[:], words[0].rearrange("p n t -> p (n t)").bitcast(I32))
 
         def load_scales(tile, scales):
-            for r in range(4):
-                nc.sync.dma_start(tile[r:P:32, :].bitcast(I32), scales[0, r:16:4, :].bitcast(I32))
+            for q in range(4):
+                nc.sync.dma_start(tile[32 * q : 32 * q + 4, :].bitcast(I32), scales[0, 4 * q : 4 * q + 4, :].bitcast(I32))
 
         raw = {}
+        raw_last = sbuf("raw_last", [P, 2, PACK * P], F32)
 
-        def load_filters(b):
-            for name, h in (("r", hr), ("i", hi)):
-                raw[name, b] = sbuf("raw_%s%d" % (name, b), [P, PACK, P], F32)
-                nc.sync.dma_start(raw[name, b][:], h[:, b * P : (b + 1) * P].rearrange("(p j) w -> p j w", j=PACK))
+        def load_filters(name, b):
+            if b == D:
+                raw[name, b] = raw_last[:, "ri".index(name), :].rearrange("p (j w) -> p j w", j=PACK)
+            else:
+                raw[name, b] = sbuf("raw_%s%d" % (name, b), [P, PACK, P], F32)[:]
+            h = hr if name == "r" else hi
+            nc.sync.dma_start(raw[name, b], h[:, b * P : (b + 1) * P].rearrange("(p j) w -> p j w", j=PACK))
 
         nc.sync.dma_start(offsets[:], offs)
-        nc.scalar.activation(root[:, :, 0:PAD], ones[:], ACT.Abs_reciprocal_sqrt, scale=0.2)
         load_words(xw, x_words)
+        nc.scalar.activation(root[:, B:, 0:PAD], ones[:, B:, :], ACT.Abs_reciprocal_sqrt, scale=0.2)
         load_scales(xs, x_scales)
-        load_filters(FIRST)
+        load_filters("r", A)
+        load_filters("i", A)
+        load_filters("i", B)
         load_words(ew, e_words)
         load_scales(es, e_scales)
-        for b in range(FIRST + 1, BANDS):
-            load_filters(b)
+        load_filters("r", B)
+        for b in (C, D):
+            load_filters("i", b)
+            load_filters("r", b)
 
         rounded = per_band("rounded", [P, 3, P * PACK], BF16)
-        words = per_band("words", [P, 3 * P], U32)
+        words = per_band("words", [P, 3 * P], U32, {C: "raw_last"})
         planes = per_band("planes", [P, 3 * P], U8)
+        place = "nri".index
 
         def interleaved(tile):
             return tile.rearrange("p (c i t) -> p c t i", i=4, t=PACK)
 
         def rows(name, b):
-            return raw[name, b][:].rearrange("p t (c i) -> p c t i", i=4)
+            return raw[name, b].rearrange("p t (c i) -> p c t i", i=4)
 
-        def round_filters(b):
-            copy = nc.vector.tensor_copy if b == LAST else nc.scalar.copy
-            for place, name in ((1, "r"), (2, "i")):
-                copy(interleaved(rounded[b][:, place, :]), rows(name, b))
+        def round_on(engine, name, b):
+            copy = nc.vector.tensor_copy if engine == "vector" else nc.scalar.copy
+            copy(interleaved(rounded[b][:, place(name), :]), rows(name, b))
+
+        def round_last():
+            nc.vector.tensor_copy(
+                rounded[D][:, 1:3, :].rearrange("p a (c i t) -> p a c t i", i=4, t=PACK),
+                raw_last[:].rearrange("p a (t c i) -> p a c t i", i=4, t=PACK),
+            )
 
         def negate(b):
-            if b == FIRST:
+            if b in (A, B):
                 nc.scalar.activation(interleaved(rounded[b][:, 0, :]), rows("i", b), ACT.Copy, scale=-1.0)
             else:
                 nc.vector.tensor_scalar(rounded[b][:, 0, :], rounded[b][:, 2, :], -1.0, None, ALU.mult)
 
-        def quantise(b, first, count):
+        def quantise(names, b):
+            first, count = place(names[0]), len(names)
             cols = slice(first * P, (first + count) * P)
             nc.vector.quantize_mx(
                 words[b][:, cols].bitcast(FP8X4), planes[b][:, cols],
                 rounded[b][:, first : first + count, :].rearrange("p n w -> p (n w)"),
             )
 
-        def quantise_band(b):
-            negate(b)
-            quantise(b, 1, 2)
-            quantise(b, 0, 1)
+        def gather(target, window, part=WHOLE):
+            dealt = target[:, part[0] : part[1]].rearrange("p (h s i) -> p h i s", s=2, i=P)
+            nc.vector.tensor_copy(dealt, window.indirect(offsets[:, part[0] // 16 : part[1] // 16]))
 
-        def gather(picked, window, lo, up):
-            dealt = picked[:, lo:up].rearrange("p (h s i) -> p h i s", s=2, i=P)
-            nc.vector.tensor_copy(dealt, window.indirect(offsets[:, lo // 16 : up // 16]))
-
-        squares = [sbuf("squares%d" % b, [P, 2 * S], F32, "raw_r%d" % MIDDLE if b == FIRST else None) for b in range(BANDS)]
-        pairs = {b: sbuf("pairs%d" % b, [P, S], F32) for b in power}
+        squares = per_band("squares", [P, 2 * S], F32, {A: "raw_r2"})
+        pairs = per_band("pairs", [P, S], F32)
         least = per_band("least", [P, S], F32)
         inverse = per_band("inverse", [P, S], F32)
         ratio = per_band("ratio", [P, S], F32)
-        result = per_band("result", [P, S], F32)
-        picked = ((xwg, xsg), (ewg, esg))
-        product, turned = {}, {}
+        result = per_band("result", [P, S], F32, {C: "least3"})
+        picked = {"x": (xwg, xsg), "e": (ewg, esg)}
+        product, passes, turned_pairs, turned_power = {}, {}, {}, {}
 
-        def multiply(b, h, table):
-            if table == 0:
-                product[b, h] = bank("product%d_%d" % (b, h), (2 * b + h) % PRODUCT_BANKS)
+        def one_pass(b, h, cols, filters, table, bins):
+            if (b, h) not in product:
+                product[b, h] = bank("product%d_%d" % (b, h), PRODUCT_BANKS[b] + h)
+                passes[b, h] = 0
+            own = (words[b][:, filters].bitcast(FP8X4), planes[b][:, filters])
+            looked_up = (picked[table][0][:, bins].bitcast(FP8X4), picked[table][1][:, bins])
+            still, moving = (looked_up, own) if b in TURNED else (own, looked_up)
+            nc.tensor.matmul_mx(
+                product[b, h][:, cols], lhsT=still[0], lhsT_scale=still[1], rhs=moving[0], rhs_scale=moving[1],
+                start=passes[b, h] == 0, stop=passes[b, h] == 3,
+            )
+            passes[b, h] = passes[b, h] + 1
+
+        def multiply_half(b, h, table):
+            first = (table == "x") * P
             for n in range(2):
-                if b == TURNED:
-                    filters = slice((1 - table) * P, (3 - table) * P)
-                    bins = slice((2 * h + n) * P, (2 * h + n + 1) * P)
+                cols = slice(n * HALF, (n + 1) * HALF)
+                if b in TURNED:
+                    block = (2 * h + n) * P
+                    one_pass(b, h, cols, slice(first, first + 2 * P), table, slice(block, block + P))
                 else:
-                    filters = slice((1 - table + n) * P, (2 - table + n) * P)
-                    bins = slice(h * HALF, (h + 1) * HALF)
-                own = (words[b][:, filters].bitcast(FP8X4), planes[b][:, filters])
-                looked_up = (picked[table][0][:, bins].bitcast(FP8X4), picked[table][1][:, bins])
-                still, moving = (looked_up, own) if b == TURNED else (own, looked_up)
-                nc.tensor.matmul_mx(
-                    product[b, h][:, n * HALF : (n + 1) * HALF],
-                    lhsT=still[0], lhsT_scale=still[1], rhs=moving[0], rhs_scale=moving[1],
-                    start=(table, n) == (0, 0), stop=(table, n) == (1, 1),
-                )
+                    one_pass(b, h, cols, slice(first + n * P, first + (n + 1) * P), table, slice(*HALVES[h]))
 
-        def multiply_band(b):
+        def multiply(b):
             for h in range(2):
-                for table in range(2):
-                    multiply(b, h, table)
-
-        def square(b):
-            for h in range(2):
-                if b == TURNED:
-                    nc.scalar.activation(squares[b][:, h * S : (h + 1) * S], product[b, h][:], ACT.Square)
-                else:
-                    target = squares[b][:].rearrange("p (part s) -> p part s", part=2)[:, :, h * HALF : (h + 1) * HALF]
-                    source = product[b, h][:].rearrange("p (part s i) -> p part i s", part=2, s=2)
-                    nc.scalar.activation(target.rearrange("p part (i s) -> p part i s", s=2), source, ACT.Square)
-
-        def turn(name, number, passes):
-            turned[name] = bank(name, number)
-            sources = [(2 * block + part, column) for block, column in passes for part in range(2)]
-            for n, (piece, column) in enumerate(sources):
-                nc.tensor.matmul(
-                    turned[name][:, column : column + P], squares[TURNED][:, piece * P : (piece + 1) * P], ident[:],
-                    start=n == 0, stop=n == len(sources) - 1, is_transpose=True,
-                )
-
-        def turn_pairs():
-            aligned = [(2 * h + s, h * P + up) for h in range(2) for s, up in ((0, 0), (1, 0), (1, HALF))]
-            turn("pairs", PRODUCT_BANKS, aligned + [(2 * h, HALF + h * P - 1) for h in range(2)])
-
-        def turn_power():
-            turn("power", PRODUCT_BANKS + 1, [(2 * h + s, s * HALF + h * P) for h in range(2) for s in range(2)])
+                for table in "xe":
+                    multiply_half(b, h, table)
 
         def in_list_order(tile):
             return tile.rearrange("p (s n) -> p n s", s=2)
 
-        def inverse_root(b, lo, up, sums):
-            nc.scalar.activation(root[:, b, PAD + lo : PAD + up], sums, ACT.Abs_reciprocal_sqrt, bias=0.2, scale=0.5)
+        def by_phase(view):
+            return view.rearrange("p (n s) -> p n s", s=2)
 
-        def parts(b):
-            return HALVES if b == LAST else WHOLE
+        def square(b, h):
+            if b in TURNED:
+                nc.scalar.activation(squares[b][:, h * S : (h + 1) * S], product[b, h][:], ACT.Square)
+            else:
+                target = squares[b][:].rearrange("p (part h i s) -> p h part i s", part=2, h=2, s=2)[:, h]
+                source = product[b, h][:].rearrange("p (part s i) -> p part i s", part=2, s=2)
+                nc.scalar.activation(target, source, ACT.Square)
 
-        def add_squares(b):
-            for lo, up in parts(b):
-                nc.vector.tensor_tensor(power[b][:, PAD + lo : PAD + up], squares[b][:, lo:up], squares[b][:, S + lo : S + up], ALU.add)
+        def turn(target, b, moves):
+            if b in SUMMED:
+                tile, sources = pairs[b], moves
+            else:
+                tile, sources = squares[b], [(2 * u + part, column) for u, column in moves for part in range(2)]
+            for n, (piece, column) in enumerate(sources):
+                nc.tensor.matmul(
+                    target[:, column : column + P], tile[:, piece * P : (piece + 1) * P], ident[:],
+                    start=n == 0, stop=n == len(sources) - 1, is_transpose=True,
+                )
 
-        def add_pairs(b):
-            for lo, up in parts(b):
-                nc.vector.tensor_tensor(pairs[b][:, lo:up], power[b][:, PAD + lo : PAD + up], power[b][:, PAD - 1 + lo : PAD - 1 + up], ALU.add)
+        def turn_pairs(b):
+            turned_pairs[b] = bank("turned_pairs%d" % b, PAIR_BANK[b])
+            aligned = [(2 * h + s, h * P + up) for h in range(2) for s, up in ((0, 0), (1, 0), (1, HALF))]
+            turn(turned_pairs[b], b, aligned + [(2 * h, HALF + h * P - 1) for h in range(2)])
 
-        def take_roots(b):
-            for lo, up in parts(b):
-                inverse_root(b, lo, up, pairs[b][:, lo:up])
+        def turn_power(b, phases):
+            if b not in turned_power:
+                turned_power[b] = bank("turned_power%d" % b, POWER_BANK[b])
+            turn(turned_power[b], b, [(u, (u % 2) * HALF + (u // 2) * P) for u in phases])
 
-        def take_least(b):
-            for lo, up in parts(b):
-                nc.vector.tensor_tensor(least[b][:, lo:up], root[:, b, PAD - 2 + lo : PAD - 2 + up], root[:, b, PAD - 4 + lo : PAD - 4 + up], ALU.min)
+        def inverse_root(target, sums):
+            nc.scalar.activation(target, sums, ACT.Abs_reciprocal_sqrt, bias=0.2, scale=0.5)
 
-        def invert(b):
-            for lo, up in parts(b):
-                nc.scalar.activation(inverse[b][:, lo:up], least[b][:, lo:up], ACT.Square)
+        def shifted(part, by):
+            return slice(part[0] + by, part[1] + by)
 
-        def divide(b):
-            for lo, up in parts(b):
-                if b == TURNED:
-                    paired = [t[b][:].rearrange("p (n s) -> p n s", s=2) for t in (ratio, inverse)]
-                    nc.vector.tensor_tensor(paired[0], in_list_order(turned["power"][:]), paired[1], ALU.mult)
-                else:
-                    nc.vector.tensor_tensor(ratio[b][:, lo:up], power[b][:, PAD + lo : PAD + up], inverse[b][:, lo:up], ALU.mult)
+        def add_squares(b, part=WHOLE):
+            nc.vector.tensor_tensor(power[:, shifted(part, PAD)], squares[b][:, shifted(part, 0)], squares[b][:, shifted(part, S)], ALU.add)
 
-        def finish(b):
-            for lo, up in parts(b):
-                if b % 2:
-                    nc.vector.tensor_scalar(result[b][:, lo:up], ratio[b][:, lo:up], -1.0, 0.0, ALU.add, ALU.max)
-                else:
-                    nc.scalar.activation(result[b][:, lo:up], ratio[b][:, lo:up], ACT.Relu, bias=-1.0)
-                nc.sync.dma_start(out[b * P : (b + 1) * P, lo:up], result[b][:, lo:up])
+        def add_turned(b):
+            both = squares[b][:].rearrange("p (u part f) -> p part u f", part=2, f=P)
+            nc.vector.tensor_tensor(pairs[b][:].rearrange("p (u f) -> p u f", f=P), both[:, 0], both[:, 1], ALU.add)
 
-        def turned_roots():
-            target = root[:, TURNED, PAD + 1 : PAD + S - 1].rearrange("p (n s) -> p n s", s=2)
-            nc.scalar.activation(target, in_list_order(turned["pairs"][:])[:, 0 : HALF - 1, :], ACT.Abs_reciprocal_sqrt, bias=0.2, scale=0.5)
-            inverse_root(TURNED, 0, 1, turned["power"][:, 0:1])
+        def add_pairs(b, part=WHOLE):
+            nc.vector.tensor_tensor(pairs[b][:, shifted(part, 0)], power[:, shifted(part, PAD)], power[:, shifted(part, PAD - 1)], ALU.add)
 
-        gather(xwg, xw[:].bitcast(U32), 0, S)
-        gather(xsg, xs[:], 0, S)
-        round_filters(FIRST)
-        negate(FIRST)
-        quantise(FIRST, 1, 2)
-        gather(ewg, ew[:].bitcast(U32), 0, S)
-        quantise(FIRST, 0, 1)
-        for h, (lo, up) in enumerate(HALVES):
-            multiply(FIRST, h, 0)
-            gather(esg, es[:], lo, up)
-            multiply(FIRST, h, 1)
-        for b in (TURNED, MIDDLE):
-            round_filters(b)
-            quantise_band(b)
+        def plain_pairs():
+            nc.vector.scalar_tensor_tensor(twice[:, PAD:], power[:, PAD:], 0.4, power[:, PAD - 1 : PAD - 1 + S], ALU.add, ALU.add)
 
-        square(FIRST)
-        add_squares(FIRST)
-        multiply_band(TURNED)
-        round_filters(LAST)
-        quantise_band(LAST)
-        add_pairs(FIRST)
-        square(TURNED)
-        multiply_band(MIDDLE)
-        take_roots(FIRST)
-        square(MIDDLE)
-        multiply_band(LAST)
-        turn_pairs()
-        take_least(FIRST)
-        add_squares(MIDDLE)
-        invert(FIRST)
-        turn_power()
-        add_pairs(MIDDLE)
-        square(LAST)
-        take_roots(MIDDLE)
-        add_squares(LAST)
-        add_pairs(LAST)
-        take_least(MIDDLE)
-        divide(FIRST)
-        take_roots(LAST)
-        turned_roots()
-        invert(MIDDLE)
-        take_least(TURNED)
-        invert(TURNED)
-        finish(FIRST)
-        divide(MIDDLE)
-        take_least(LAST)
-        finish(MIDDLE)
-        invert(LAST)
-        for b in (TURNED, LAST):
-            divide(b)
-            finish(b)
+        def plain_greater():
+            nc.vector.tensor_tensor(pairs[A][:], twice[:, PAD - 2 : PAD - 2 + S], twice[:, PAD - 4 : PAD - 4 + S], ALU.max)
+
+        def plain_root():
+            nc.scalar.activation(least[A][:], pairs[A][:], ACT.Abs_reciprocal_sqrt, scale=0.5)
+
+        def plain_excess():
+            nc.vector.scalar_tensor_tensor(ratio[A][:], pairs[A][:], -0.5, power[:, PAD:], ALU.mult, ALU.add)
+
+        def plain_finish():
+            nc.vector.scalar_tensor_tensor(result[A][:], ratio[A][:], 0.0, inverse[A][:], ALU.max, ALU.mult)
+            nc.sync.dma_start(out[0:P, :], result[A][:])
+
+        def take_roots(b, part=WHOLE):
+            if b in TURNED:
+                source = in_list_order(turned_pairs[b][:])[:, part[0] // 2 : part[1] // 2, :]
+                inverse_root(by_phase(root[:, b, shifted(part, PAD + 1)]), source)
+            else:
+                inverse_root(root[:, b, shifted(part, PAD)], pairs[b][:, shifted(part, 0)])
+
+        def first_root(b):
+            inverse_root(root[:, b, PAD : PAD + 1], turned_power[b][:, 0:1])
+
+        def take_least(b, part=WHOLE):
+            nc.vector.tensor_tensor(least[b][:, shifted(part, 0)], root[:, b, shifted(part, PAD - 2)], root[:, b, shifted(part, PAD - 4)], ALU.min)
+
+        def invert(b, part=WHOLE, engine="scalar"):
+            cols = shifted(part, 0)
+            if engine == "vector":
+                nc.vector.tensor_tensor(inverse[b][:, cols], least[b][:, cols], least[b][:, cols], ALU.mult)
+            else:
+                nc.scalar.activation(inverse[b][:, cols], least[b][:, cols], ACT.Square)
+
+        def divide(b, part=WHOLE):
+            cols = shifted(part, 0)
+            if b in TURNED:
+                source = in_list_order(turned_power[b][:])[:, part[0] // 2 : part[1] // 2, :]
+                nc.vector.tensor_tensor(by_phase(ratio[b][:, cols]), source, by_phase(inverse[b][:, cols]), ALU.mult)
+            else:
+                nc.vector.tensor_tensor(ratio[b][:, cols], power[:, shifted(part, PAD)], inverse[b][:, cols], ALU.mult)
+
+        def finish(engine, b, part=WHOLE):
+            cols = shifted(part, 0)
+            if engine == "vector":
+                nc.vector.tensor_scalar(result[b][:, cols], ratio[b][:, cols], -1.0, 0.0, ALU.add, ALU.max)
+            else:
+                nc.scalar.activation(result[b][:, cols], ratio[b][:, cols], ACT.Relu, bias=-1.0)
+            queue = nc.scalar if b == C else nc.sync
+            queue.dma_start(out[b * P : (b + 1) * P, cols], result[b][:, cols])
+
+        low, high = HALVES
+        gather(xwg, xw[:].bitcast(U32))
+        gather(xsg, xs[:])
+        round_on("scalar", "r", A)
+        round_on("scalar", "i", A)
+        negate(A)
+        quantise("ri", A)
+        gather(ewg, ew[:].bitcast(U32))
+        quantise("n", A)
+        for h in range(2):
+            multiply_half(A, h, "x")
+            gather(esg, es[:], HALVES[h])
+            multiply_half(A, h, "e")
+        round_on("scalar", "i", B)
+        negate(B)
+        round_on("scalar", "r", B)
+        round_on("scalar", "i", C)
+        round_on("scalar", "r", C)
+        quantise("nri", B)
+        multiply(B)
+        negate(C)
+        round_last()
+        quantise("nri", C)
+        multiply(C)
+        square(A, 0)
+        square(A, 1)
+        negate(D)
+        add_squares(A)
+        quantise("nri", D)
+        multiply(D)
+        square(B, 0)
+        square(B, 1)
+        plain_pairs()
+        square(C, 0)
+        square(C, 1)
+        add_turned(B)
+        turn_pairs(B)
+        turn_power(B, [0])
+        plain_greater()
+        add_turned(C)
+        turn_pairs(C)
+        turn_power(C, [0])
+        square(D, 0)
+        square(D, 1)
+        plain_root()
+        plain_excess()
+        take_roots(B)
+        first_root(B)
+        invert(A)
+        add_turned(D)
+        turn_pairs(D)
+        turn_power(D, [0])
+        turn_power(B, [1, 2, 3])
+        take_least(B)
+        take_roots(C)
+        first_root(C)
+        turn_power(C, [1, 2, 3])
+        plain_finish()
+        invert(B)
+        take_least(C)
+        take_roots(D)
+        first_root(D)
+        turn_power(D, [1, 2, 3])
+        divide(B)
+        invert(C)
+        take_least(D, low)
+        take_least(D, high)
+        divide(C)
+        finish("vector", B)
+        invert(D, low)
+        invert(D, high)
+        finish("scalar", C)
+        divide(D, low)
+        divide(D, high)
+        finish("vector", D, low)
+        finish("vector", D, high)

@@ -90,16 +90,14 @@ def tile_picked_ycfar_go_p_kernel(
         load_scales(xs, x_scales)
         load_filters("r", A)
         load_filters("i", A)
-        load_filters("i", B)
         load_words(ew, e_words)
         load_scales(es, e_scales)
-        load_filters("r", B)
-        for b in (C, D):
-            load_filters("i", b)
+        for b in (B, C, D):
             load_filters("r", b)
+            load_filters("i", b)
 
         rounded = per_band("rounded", [P, 3, P * PACK], BF16)
-        words = per_band("words", [P, 3 * P], U32, {C: "raw_last"})
+        words = per_band("words", [P, 3 * P], U32)
         planes = per_band("planes", [P, 3 * P], U8)
         place = "nri".index
 
@@ -120,7 +118,7 @@ def tile_picked_ycfar_go_p_kernel(
             )
 
         def negate(b):
-            if b in (A, B):
+            if b == A:
                 nc.scalar.activation(interleaved(rounded[b][:, 0, :]), rows("i", b), ACT.Copy, scale=-1.0)
             else:
                 nc.vector.tensor_scalar(rounded[b][:, 0, :], rounded[b][:, 2, :], -1.0, None, ALU.mult)
@@ -275,8 +273,7 @@ def tile_picked_ycfar_go_p_kernel(
                 nc.vector.tensor_scalar(result[b][:, cols], ratio[b][:, cols], -1.0, 0.0, ALU.add, ALU.max)
             else:
                 nc.scalar.activation(result[b][:, cols], ratio[b][:, cols], ACT.Relu, bias=-1.0)
-            queue = nc.scalar if b == C else nc.sync
-            queue.dma_start(out[b * P : (b + 1) * P, cols], result[b][:, cols])
+            nc.sync.dma_start(out[b * P : (b + 1) * P, cols], result[b][:, cols])
 
         low, high = HALVES
         gather(xwg, xw[:].bitcast(U32))
@@ -291,22 +288,21 @@ def tile_picked_ycfar_go_p_kernel(
             multiply_half(A, h, "x")
             gather(esg, es[:], HALVES[h])
             multiply_half(A, h, "e")
-        round_on("scalar", "i", B)
-        negate(B)
-        round_on("scalar", "r", B)
-        round_on("scalar", "i", C)
-        round_on("scalar", "r", C)
-        quantise("nri", B)
-        multiply(B)
-        negate(C)
-        round_last()
-        quantise("nri", C)
-        multiply(C)
+        for b in (B, C):
+            round_on("scalar", "r", b)
+            round_on("scalar", "i", b)
+            negate(b)
+            quantise("ri", b)
+            quantise("n", b)
+            multiply(b)
         square(A, 0)
         square(A, 1)
-        negate(D)
+        round_on("vector", "r", D)
+        round_on("vector", "i", D)
         add_squares(A)
-        quantise("nri", D)
+        negate(D)
+        quantise("ri", D)
+        quantise("n", D)
         multiply(D)
         square(B, 0)
         square(B, 1)

@@ -138,7 +138,7 @@ def tile_picked_ycfar_go_p_kernel(
         squares = per_band("squares", [P, 2 * S], F32, {A: "raw_r2"})
         pairs = per_band("pairs", [P, S], F32)
         least = per_band("least", [P, S], F32)
-        inverse = per_band("inverse", [P, S], F32)
+        inverse = per_band("inverse", [P, S], F32, {A: "pairs0"})
         ratio = per_band("ratio", [P, S], F32)
         result = per_band("result", [P, S], F32, {C: "least3"})
         picked = {"x": (xwg, xsg), "e": (ewg, esg)}
@@ -171,6 +171,15 @@ def tile_picked_ycfar_go_p_kernel(
             for h in range(2):
                 for table in "xe":
                     multiply_half(b, h, table)
+
+        def keep_warm(passes):
+            own = (words[D][:].bitcast(FP8X4), planes[D][:])
+            spare = bank("spare", POWER_BANK[B])
+            for n in range(passes):
+                nc.tensor.matmul_mx(
+                    spare[:, 0:HALF], lhsT=own[0][:, 0:P], lhsT_scale=own[1][:, 0:P],
+                    rhs=own[0][:, 0:HALF], rhs_scale=own[1][:, 0:HALF], start=n == 0, stop=n == passes - 1,
+                )
 
         def in_list_order(tile):
             return tile.rearrange("p (s n) -> p n s", s=2)
@@ -304,6 +313,7 @@ def tile_picked_ycfar_go_p_kernel(
         quantise("ri", D)
         quantise("n", D)
         multiply(D)
+        keep_warm(2)
         square(B, 0)
         square(B, 1)
         plain_pairs()

@@ -172,9 +172,9 @@ def tile_picked_ycfar_go_p_kernel(
                 for table in "xe":
                     multiply_half(b, h, table)
 
-        def keep_warm(passes):
+        def keep_warm(passes, number):
             own = (words[D][:].bitcast(FP8X4), planes[D][:])
-            spare = bank("spare", POWER_BANK[B])
+            spare = bank("spare%d" % number, number)
             for n in range(passes):
                 nc.tensor.matmul_mx(
                     spare[:, 0:HALF], lhsT=own[0][:, 0:P], lhsT_scale=own[1][:, 0:P],
@@ -313,7 +313,7 @@ def tile_picked_ycfar_go_p_kernel(
         quantise("ri", D)
         quantise("n", D)
         multiply(D)
-        keep_warm(2)
+        keep_warm(1, POWER_BANK[B])
         square(B, 0)
         square(B, 1)
         plain_pairs()
@@ -322,10 +322,12 @@ def tile_picked_ycfar_go_p_kernel(
         add_turned(B)
         turn_pairs(B)
         turn_power(B, [0])
+        keep_warm(1, PRODUCT_BANKS[D])
         plain_greater()
         add_turned(C)
         turn_pairs(C)
         turn_power(C, [0])
+        keep_warm(1, PRODUCT_BANKS[D] + 1)
         square(D, 0)
         square(D, 1)
         plain_root()

@@ -172,15 +172,6 @@ def tile_picked_ycfar_go_p_kernel(
                 for table in "xe":
                     multiply_half(b, h, table)
 
-        def keep_warm(passes, number):
-            own = (words[D][:].bitcast(FP8X4), planes[D][:])
-            spare = bank("spare%d" % number, number)
-            for n in range(passes):
-                nc.tensor.matmul_mx(
-                    spare[:, 0:HALF], lhsT=own[0][:, 0:P], lhsT_scale=own[1][:, 0:P],
-                    rhs=own[0][:, 0:HALF], rhs_scale=own[1][:, 0:HALF], start=n == 0, stop=n == passes - 1,
-                )
-
         def in_list_order(tile):
             return tile.rearrange("p (s n) -> p n s", s=2)
 
@@ -313,7 +304,6 @@ def tile_picked_ycfar_go_p_kernel(
         quantise("ri", D)
         quantise("n", D)
         multiply(D)
-        keep_warm(1, POWER_BANK[B])
         square(B, 0)
         square(B, 1)
         plain_pairs()
@@ -322,12 +312,10 @@ def tile_picked_ycfar_go_p_kernel(
         add_turned(B)
         turn_pairs(B)
         turn_power(B, [0])
-        keep_warm(1, PRODUCT_BANKS[D])
         plain_greater()
         add_turned(C)
         turn_pairs(C)
         turn_power(C, [0])
-        keep_warm(1, PRODUCT_BANKS[D] + 1)
         square(D, 0)
         square(D, 1)
         plain_root()

@@ -108,8 +108,14 @@ def tile_picked_ycfar_go_p_kernel(
             return raw[name, b].rearrange("p t (c i) -> p c t i", i=4)
 
         def round_on(engine, name, b):
-            copy = nc.vector.tensor_copy if engine == "vector" else nc.scalar.copy
-            copy(interleaved(rounded[b][:, place(name), :]), rows(name, b))
+            target = rounded[b][:, place(name), :]
+            if engine == "vector":
+                nc.vector.tensor_copy(interleaved(target), rows(name, b))
+            else:
+                nc.scalar.copy(
+                    target.rearrange("p (c i u t) -> p c u i t", i=4, u=2, t=2),
+                    raw[name, b].rearrange("p (u t) (c i) -> p c u i t", i=4, t=2),
+                )
 
         def round_last():
             nc.vector.tensor_copy(

from contextlib import ExitStack

import concourse.mybir as mybir
from concourse.masks import make_identity

K, T, S, V = 512, 1024, 512, 512
FLOPS = 4 * 2 * K * V * S

F32 = mybir.dt.float32
BF16 = mybir.dt.bfloat16
I32 = mybir.dt.int32
U32 = mybir.dt.uint32
U16 = mybir.dt.uint16
U8 = mybir.dt.uint8
FP8X4 = mybir.dt.float8_e4m3fn_x4
ALU = mybir.AluOpType
ACT = mybir.ActivationFunctionType

P = 128
PACK = 4
BANDS = V // P
HALF = S // 2
PAD = 4
A, B, C, D = range(BANDS)
TURNED = (B, C, D)
SUMMED = (B, C, D)
WHOLE = (0, S)
HALVES = ((0, HALF), (HALF, S))
PRODUCT_BANKS = {A: 0, B: 2, C: 4, D: 0}
PAIR_BANK = {B: 6, C: 2, D: 4}
POWER_BANK = {B: 7, C: 3, D: 5}


def tile_picked_ycfar_go_p_kernel(
    tc, x_words, x_scales, e_words, e_scales, hr, hi, offs, out
):
    nc = tc.nc
    with ExitStack() as ctx:
        keep = ctx.enter_context(tc.tile_pool(name="keep", bufs=1))
        psum = ctx.enter_context(tc.psum_pool(name="psum", bufs=1))

        def sbuf(name, shape, dtype, over=None):
            return keep.tile(shape, dtype, name=name, tag=over or name, align_bytes=64)

        def bank(name, number):
            return psum.tile([P, S], F32, name=name, tag="bank%d" % number)

        def per_band(name, shape, dtype, over=None):
            return [sbuf("%s%d" % (name, b), shape, dtype, (over or {}).get(b)) for b in range(BANDS)]

        offsets = keep.tile([P, S // 16], U16, name="offsets")
        xw, ew = sbuf("xw", [P, T], I32), sbuf("ew", [P, T], I32)
        xs, es = sbuf("xs", [P, T], U8), sbuf("es", [P, T], U8)
        xwg, ewg = sbuf("xwg", [P, S], U32), sbuf("ewg", [P, S], U32)
        xsg, esg = sbuf("xsg", [P, S], U8), sbuf("esg", [P, S], U8)
        ones = sbuf("ones", [P, BANDS, PAD], F32)
        root = sbuf("root", [P, BANDS, PAD + S + PAD], F32)
        ident = sbuf("ident", [P, P], F32)
        power = sbuf("power", [P, PAD + S], F32)
        twice = sbuf("twice", [P, PAD + S], F32)

        nc.vector.memset(xs[:].bitcast(I32), 0)
        nc.vector.memset(ones[:], 1.0)
        nc.vector.memset(es[:].bitcast(I32), 0)
        nc.vector.memset(power[:, 0:PAD], 0.0)
        nc.vector.tensor_scalar(twice[:, 0:PAD], ones[:, 0, :], 0.4, None, ALU.mult)
        make_identity(nc, ident[:])

        def load_words(tile, words):
            nc.sync.dma_start(tile[:], words[0].rearrange("p n t -> p (n t)").bitcast(I32))

        def load_scales(tile, scales):
            for q in range(4):
                nc.sync.dma_start(tile[32 * q : 32 * q + 4, :].bitcast(I32), scales[0, 4 * q : 4 * q + 4, :].bitcast(I32))

        raw = {}
        raw_last = sbuf("raw_last", [P, 2, PACK * P], F32)

        def load_filters(name, b):
            if b == D:
                raw[name, b] = raw_last[:, "ri".index(name), :].rearrange("p (j w) -> p j w", j=PACK)
            else:
                raw[name, b] = sbuf("raw_%s%d" % (name, b), [P, PACK, P], F32)[:]
            h = hr if name == "r" else hi
            nc.sync.dma_start(raw[name, b], h[:, b * P : (b + 1) * P].rearrange("(p j) w -> p j w", j=PACK))

        nc.sync.dma_start(offsets[:], offs)
        load_words(xw, x_words)
        nc.scalar.activation(root[:, B:, 0:PAD], ones[:, B:, :], ACT.Abs_reciprocal_sqrt, scale=0.2)
        load_scales(xs, x_scales)
        load_filters("r", A)
        load_filters("i", A)
        load_words(ew, e_words)
        load_scales(es, e_scales)
        for b in (B, C, D):
            load_filters("r", b)
            load_filters("i", b)

        rounded = per_band("rounded", [P, 3, P * PACK], BF16)
        words = per_band("words", [P, 3 * P], U32)
        planes = per_band("planes", [P, 3 * P], U8)
        place = "nri".index

        def interleaved(tile):
            return tile.rearrange("p (c i t) -> p c t i", i=4, t=PACK)

        def rows(name, b):
            return raw[name, b].rearrange("p t (c i) -> p c t i", i=4)

        def round_on(engine, name, b):
            target = rounded[b][:, place(name), :]
            if engine == "vector":
                nc.vector.tensor_copy(interleaved(target), rows(name, b))
            else:
                nc.scalar.copy(
                    target.rearrange("p (c i u t) -> p c u i t", i=4, u=2, t=2),
                    raw[name, b].rearrange("p (u t) (c i) -> p c u i t", i=4, t=2),
                )

        def round_last():
            nc.vector.tensor_copy(
                rounded[D][:, 1:3, :].rearrange("p a (c i t) -> p a c t i", i=4, t=PACK),
                raw_last[:].rearrange("p a (t c i) -> p a c t i", i=4, t=PACK),
            )

        def negate(b):
            if b == A:
                nc.scalar.activation(interleaved(rounded[b][:, 0, :]), rows("i", b), ACT.Copy, scale=-1.0)
            else:
                nc.vector.tensor_scalar(rounded[b][:, 0, :], rounded[b][:, 2, :], -1.0, None, ALU.mult)

        def quantise(names, b):
            first, count = place(names[0]), len(names)
            cols = slice(first * P, (first + count) * P)
            nc.vector.quantize_mx(
                words[b][:, cols].bitcast(FP8X4), planes[b][:, cols],
                rounded[b][:, first : first + count, :].rearrange("p n w -> p (n w)"),
            )

        def gather(target, window, part=WHOLE):
            dealt = target[:, part[0] : part[1]].rearrange("p (h s i) -> p h i s", s=2, i=P)
            nc.vector.tensor_copy(dealt, window.indirect(offsets[:, part[0] // 16 : part[1] // 16]))

        squares = per_band("squares", [P, 2 * S], F32, {A: "raw_r2"})
        pairs = per_band("pairs", [P, S], F32)
        least = per_band("least", [P, S], F32)
        inverse = per_band("inverse", [P, S], F32, {A: "pairs0"})
        ratio = per_band("ratio", [P, S], F32)
        result = per_band("result", [P, S], F32, {C: "least3"})
        picked = {"x": (xwg, xsg), "e": (ewg, esg)}
        product, passes, turned_pairs, turned_power = {}, {}, {}, {}

        def one_pass(b, h, cols, filters, table, bins):
            if (b, h) not in product:
                product[b, h] = bank("product%d_%d" % (b, h), PRODUCT_BANKS[b] + h)
                passes[b, h] = 0
            own = (words[b][:, filters].bitcast(FP8X4), planes[b][:, filters])
            looked_up = (picked[table][0][:, bins].bitcast(FP8X4), picked[table][1][:, bins])
            still, moving = (looked_up, own) if b in TURNED else (own, looked_up)
            nc.tensor.matmul_mx(
                product[b, h][:, cols], lhsT=still[0], lhsT_scale=still[1], rhs=moving[0], rhs_scale=moving[1],
                start=passes[b, h] == 0, stop=passes[b, h] == 3,
            )
            passes[b, h] = passes[b, h] + 1

        def multiply_half(b, h, table):
            first = (table == "x") * P
            for n in range(2):
                cols = slice(n * HALF, (n + 1) * HALF)
                if b in TURNED:
                    block = (2 * h + n) * P
                    one_pass(b, h, cols, slice(first, first + 2 * P), table, slice(block, block + P))
                else:
                    one_pass(b, h, cols, slice(first + n * P, first + (n + 1) * P), table, slice(*HALVES[h]))

        def multiply(b):
            for h in range(2):
                for table in "xe":
                    multiply_half(b, h, table)

        def in_list_order(tile):
            return tile.rearrange("p (s n) -> p n s", s=2)

        def by_phase(view):
            return view.rearrange("p (n s) -> p n s", s=2)

        def square(b, h):
            if b in TURNED:
                nc.scalar.activation(squares[b][:, h * S : (h + 1) * S], product[b, h][:], ACT.Square)
            else:
                target = squares[b][:].rearrange("p (part h i s) -> p h part i s", part=2, h=2, s=2)[:, h]
                source = product[b, h][:].rearrange("p (part s i) -> p part i s", part=2, s=2)
                nc.scalar.activation(target, source, ACT.Square)

        def turn(target, b, moves):
            if b in SUMMED:
                tile, sources = pairs[b], moves
            else:
                tile, sources = squares[b], [(2 * u + part, column) for u, column in moves for part in range(2)]
            for n, (piece, column) in enumerate(sources):
                nc.tensor.matmul(
                    target[:, column : column + P], tile[:, piece * P : (piece + 1) * P], ident[:],
                    start=n == 0, stop=n == len(sources) - 1, is_transpose=True,
                )

        def turn_pairs(b):
            turned_pairs[b] = bank("turned_pairs%d" % b, PAIR_BANK[b])
            aligned = [(2 * h + s, h * P + up) for h in range(2) for s, up in ((0, 0), (1, 0), (1, HALF))]
            turn(turned_pairs[b], b, aligned + [(2 * h, HALF + h * P - 1) for h in range(2)])

        def turn_power(b, phases):
            if b not in turned_power:
                turned_power[b] = bank("turned_power%d" % b, POWER_BANK[b])
            turn(turned_power[b], b, [(u, (u % 2) * HALF + (u // 2) * P) for u in phases])

        def inverse_root(target, sums):
            nc.scalar.activation(target, sums, ACT.Abs_reciprocal_sqrt, bias=0.2, scale=0.5)

        def shifted(part, by):
            return slice(part[0] + by, part[1] + by)

        def add_squares(b, part=WHOLE):
            nc.vector.tensor_tensor(power[:, shifted(part, PAD)], squares[b][:, shifted(part, 0)], squares[b][:, shifted(part, S)], ALU.add)

        def add_turned(b):
            both = squares[b][:].rearrange("p (u part f) -> p part u f", part=2, f=P)
            nc.vector.tensor_tensor(pairs[b][:].rearrange("p (u f) -> p u f", f=P), both[:, 0], both[:, 1], ALU.add)

        def add_pairs(b, part=WHOLE):
            nc.vector.tensor_tensor(pairs[b][:, shifted(part, 0)], power[:, shifted(part, PAD)], power[:, shifted(part, PAD - 1)], ALU.add)

        def plain_pairs():
            nc.vector.scalar_tensor_tensor(twice[:, PAD:], power[:, PAD:], 0.4, power[:, PAD - 1 : PAD - 1 + S], ALU.add, ALU.add)

        def plain_greater():
            nc.vector.tensor_tensor(pairs[A][:], twice[:, PAD - 2 : PAD - 2 + S], twice[:, PAD - 4 : PAD - 4 + S], ALU.max)

        def plain_root():
            nc.scalar.activation(least[A][:], pairs[A][:], ACT.Abs_reciprocal_sqrt, scale=0.5)

        def plain_excess():
            nc.vector.scalar_tensor_tensor(ratio[A][:], pairs[A][:], -0.5, power[:, PAD:], ALU.mult, ALU.add)

        def plain_finish():
            nc.vector.scalar_tensor_tensor(result[A][:], ratio[A][:], 0.0, inverse[A][:], ALU.max, ALU.mult)
            nc.sync.dma_start(out[0:P, :], result[A][:])

        def take_roots(b, part=WHOLE):
            if b in TURNED:
                source = in_list_order(turned_pairs[b][:])[:, part[0] // 2 : part[1] // 2, :]
                inverse_root(by_phase(root[:, b, shifted(part, PAD + 1)]), source)
            else:
                inverse_root(root[:, b, shifted(part, PAD)], pairs[b][:, shifted(part, 0)])

        def first_root(b):
            inverse_root(root[:, b, PAD : PAD + 1], turned_power[b][:, 0:1])

        def take_least(b, part=WHOLE):
            nc.vector.tensor_tensor(least[b][:, shifted(part, 0)], root[:, b, shifted(part, PAD - 2)], root[:, b, shifted(part, PAD - 4)], ALU.min)

        def invert(b, part=WHOLE, engine="scalar"):
            cols = shifted(part, 0)
            if engine == "vector":
                nc.vector.tensor_tensor(inverse[b][:, cols], least[b][:, cols], least[b][:, cols], ALU.mult)
            else:
                nc.scalar.activation(inverse[b][:, cols], least[b][:, cols], ACT.Square)

        def divide(b, part=WHOLE):
            cols = shifted(part, 0)
            if b in TURNED:
                source = in_list_order(turned_power[b][:])[:, part[0] // 2 : part[1] // 2, :]
                nc.vector.tensor_tensor(by_phase(ratio[b][:, cols]), source, by_phase(inverse[b][:, cols]), ALU.mult)
            else:
                nc.vector.tensor_tensor(ratio[b][:, cols], power[:, shifted(part, PAD)], inverse[b][:, cols], ALU.mult)

        def finish(engine, b, part=WHOLE):
            cols = shifted(part, 0)
            if engine == "vector":
                nc.vector.tensor_scalar(result[b][:, cols], ratio[b][:, cols], -1.0, 0.0, ALU.add, ALU.max)
            else:
                nc.scalar.activation(result[b][:, cols], ratio[b][:, cols], ACT.Relu, bias=-1.0)
            nc.sync.dma_start(out[b * P : (b + 1) * P, cols], result[b][:, cols])

        low, high = HALVES
        gather(xwg, xw[:].bitcast(U32))
        gather(xsg, xs[:])
        round_on("scalar", "r", A)
        round_on("scalar", "i", A)
        negate(A)
        quantise("ri", A)
        gather(ewg, ew[:].bitcast(U32))
        quantise("n", A)
        for h in range(2):
            multiply_half(A, h, "x")
            gather(esg, es[:], HALVES[h])
            multiply_half(A, h, "e")
        for b in (B, C):
            round_on("scalar", "r", b)
            round_on("scalar", "i", b)
            negate(b)
            quantise("ri", b)
            quantise("n", b)
            multiply(b)
        square(A, 0)
        square(A, 1)
        round_on("vector", "r", D)
        round_on("vector", "i", D)
        add_squares(A)
        negate(D)
        quantise("ri", D)
        quantise("n", D)
        multiply(D)
        square(B, 0)
        square(B, 1)
        plain_pairs()
        square(C, 0)
        square(C, 1)
        add_turned(B)
        turn_pairs(B)
        turn_power(B, [0])
        plain_greater()
        add_turned(C)
        turn_pairs(C)
        turn_power(C, [0])
        square(D, 0)
        square(D, 1)
        plain_root()
        plain_excess()
        take_roots(B)
        first_root(B)
        invert(A)
        add_turned(D)
        turn_pairs(D)
        turn_power(D, [0])
        turn_power(B, [1, 2, 3])
        take_least(B)
        take_roots(C)
        first_root(C)
        turn_power(C, [1, 2, 3])
        plain_finish()
        invert(B)
        take_least(C)
        take_roots(D)
        first_root(D)
        turn_power(D, [1, 2, 3])
        divide(B)
        invert(C)
        take_least(D, low)
        take_least(D, high)
        divide(C)
        finish("vector", B)
        invert(D, low)
        invert(D, high)
        finish("scalar", C)
        divide(D, low)
        divide(D, high)
        finish("vector", D, low)
        finish("vector", D, high)
